import numpy as np, ml_dtypes
CORES = [3,7,11,15,131,135,139,143]
N = 8
BF = ml_dtypes.bfloat16
S, L, CAP, RO, KM = 2048, 256, 48, 5, 3967
W = S + RO * CAP
def joined(c, T):
    e = np.add.accumulate(4 + (c & 3), axis=1)
    j = np.minimum(np.sum(e[:, :, None] <= (5 * np.arange(L) + 2)[None, None, :], axis=1), L - 2)
    p = np.take_along_axis(c, j, 1); q = np.take_along_axis(c, j + 1, 1)
    left = np.take_along_axis(T, p[:, None, :], 2)[:, 8:]; right = np.take_along_axis(T, q[:, None, :], 2)[:, :8]
    return p, np.concatenate([left, right], axis=1).astype(np.int64)
def places(z, w, k):
    u = np.sum(z * w[:, :, 0:1], axis=1) & (S - 1); v = np.sum(z * w[:, :, 1:2], axis=1) & (S - 1)
    return (((u * v) >> 5)[:, None, :] + k[:, :, None] * u[:, None, :]) & (S - 1)
def probe(z, w, k, b, U):
    h = places(z, w, k)
    d = np.stack([np.sum(np.abs(np.take_along_axis(U, h[:, m:m + 1], 2) - z), axis=1) for m in range(16)], axis=1)
    m = np.argmin(d, axis=1)[:, None, :]
    return np.take_along_axis(h, m, 1)[:, 0], np.take_along_axis(d, m, 1)[:, 0] < b[:, None]
def lowest(h, fit):
    win = np.zeros(fit.shape, bool)
    for g in range(8):
        i = np.flatnonzero(fit[g]); win[g, i[np.unique(h[g, i], return_index=True)[1]]] = True
    return win
def parts(rng):
    return (rng.integers(0, 256, (N, 8, 16, S), dtype=np.int16), rng.integers(0, 256, (N, 8, 16, S), dtype=np.int16), rng.integers(0, S, (N, 8, L)),
            rng.integers(0, 4096, (N, 8, 16, 2)), rng.integers(0, KM + 1, (N, 8, 16)), rng.integers(840, 1040, (N, 8)))
def pack(us, tp, c, w, k, th):
    return {"us": us.reshape(N, 128, S).astype(np.float32).astype(BF), "tp": tp.reshape(N, 128, S).astype(np.float32).astype(BF), "c0": np.ascontiguousarray(c).astype(np.int32),
            "hw": np.ascontiguousarray(w.reshape(N, 128, 2)).astype(np.int32), "km": np.ascontiguousarray(k.reshape(N, 128, 1)).astype(np.int32), "th": np.ascontiguousarray(th.reshape(N, 8, 1)).astype(np.int32)}
def setup_inputs(rng):
    return pack(*parts(rng))
def near(z, d):
    a = d[None, :] // 16 + (np.arange(16)[:, None] < d[None, :] % 16)
    return np.where(z < 128, z + a, z - a)
def setup_inputs_corners(rng):
    us, tp, c, w, k, th = parts(rng); w[:, :, 0, 0] |= 1; cnt = (0, 1, CAP - 1, CAP, CAP + 1, L); used = {}; sent = {}; zs = []
    def plant(q, g, h, z, todo):
        st, sl, ds = [], [], []
        for i, d in todo:
            r = int(rng.integers(0, 16)); cand = h[:, i].tolist()
            for m in range(16):
                s = cand[(m + r) % 16]
                if s not in used[q, g]:
                    used[q, g].add(s); st.append(s); sl.append(i); ds.append(d); break
        if st: us[q, g][:, np.array(st)] = near(z[:, np.array(sl)], np.array(ds))
    for q in range(N):
        for g in range(8):
            v = (g + q) % 8; used[q, g] = set()
            if v == 6: c[q, g] = 4 * rng.integers(0, S // 4, L) + 3; c[q, g, :3] = S - 1
            elif v == 7: c[q, g] = 4 * rng.integers(0, S // 4, L); c[q, g, L - 3:] = 0
            else: c[q, g] = 4 * rng.permutation(S // 4)[:L] + 1; k[q, g] = rng.permutation(min(S, KM + 1))[:16]; th[q, g] = rng.choice(np.array([1, 2, 64, 100]))
            if v in (1, 2, 3): us[q, g, :, 0] = 0; used[q, g].add(0)
        p, z = joined(c[q], tp[q]); even = (np.sum(z * w[q, :, :, 0:1], axis=1) & 1) == 0
        for g in range(8):
            if (g + q) % 8 < 6: tp[q, g, 8, np.unique(p[g, even[g]])] ^= 1
        p, z = joined(c[q], tp[q]); zs.append(z); h = places(z, w[q], k[q])
        for g in range(8):
            v = (g + q) % 8
            if v > 5: continue
            n = cnt[v]; pair = 2 if n >= 2 else 0; front = rng.permutation(L - 2).tolist(); t = int(th[q, g])
            poor = front[:n - pair] + ([L - 2, L - 1] if pair else []); fits = front[n - pair:] + ([] if pair else [L - 2])
            plant(q, g, h[g], z[g], [(i, (t - 1) * int(rng.integers(0, 2))) for i in fits] + [(i, t) for i in poor if i < L - 1 and rng.random() < 0.5])
            sent[q, g] = sorted(poor)[:CAP]
    for q in range(N):
        a = (q + 1) % N; h = places(zs[q], w[a], k[a])
        for g in range(8):
            if (q, g) in sent:
                t = int(th[a, g]); full = (g + q) % 8 == 4
                plant(a, g, h[g], zs[q][g], [(i, (0, t - 1, t)[int(rng.integers(0, 2 if full else 3))]) for i in sent[q, g] if i < L - 1 and (full or rng.random() < 0.6)])
    return pack(us, tp, c, w, k, th)
def setup_inputs_ends(rng):
    us = 255 * rng.integers(0, 2, (N, 8, 16, S), dtype=np.int16); tp = 255 * rng.integers(0, 2, (N, 8, 16, S), dtype=np.int16)
    inner = np.argsort(rng.random((N, 8, L)), axis=-1) < 5 * L // 16; anyc = rng.integers(0, S, (N, 8, L)); roll = rng.random((N, 8, L))
    w = 4095 * rng.integers(0, 2, (N, 8, 16, 2)); w[:, :, 0, 0] = 0; w[:, :, 1, 0] = 4095
    k = np.where(np.argsort(rng.random((N, 8, 16)), axis=-1) < 4, rng.integers(0, KM + 1, (N, 8, 16)), KM * rng.integers(0, 2, (N, 8, 16)))
    th = np.stack([4080 * (rng.permutation(8) % 2) for q in range(N)]); big = np.stack([rng.permutation(8) < 4 for q in range(N)]); big[:, 7] = True; big[0, 0] = True
    if th[N - 1, 7] == 0: th[N - 1, int(np.argmax(th[N - 1]))] = 0; th[N - 1, 7] = 4080
    c = np.where(inner, anyc, (S - 1) * (roll < 0.5)); base = ((S - 1) ** 2 >> 5) & (S - 1); one = np.zeros(16, np.int16); one[0] = 1
    for q in range(N):
        for g in range(8):
            if not big[q, g]: continue
            w[q, g] = 4095; us[q, g, :, 0] = 255; tp[q, g, :, 0] = 255; tp[q, g, :, S - 1] = 0; tp[q, g, :, S - 2] = 0; tp[q, g, 8, S - 2] = 1
            far = (S - 1, 1, 2) if g == 7 or rng.random() < 0.5 else (2, S - 1, 1)
            for lane, s in zip((1, 14, 15), far): k[q, g, lane] = (base - s) & (S - 1); us[q, g, :, s] = one
            k[q, g, 0] = 0; k[q, g, 2] = KM
            c[q, g] = np.where(inner[q, g], anyc[q, g] // 4 * 4, (S - 1) * (roll[q, g] < 0.2))
            if rng.random() < 0.5: c[q, g, 0] = S - 2; c[q, g, 1] = S - 1
            c[q, g, 4:6] = S - 1; c[q, g, 6:9] = 0; c[q, g, L - 2] = S - 2; c[q, g, L - 1] = S - 1
    return pack(us, tp, c, w, k, th)
def setup_inputs_refuse(rng):
    d = setup_inputs_ends(rng); d["th"][1] = 0
    return d
def setup_inputs_spread(rng):
    us, tp, c, w, k, th = parts(rng)
    def stones():
        v = np.floor(np.exp2(8 * rng.random((N, 8, 1, S), dtype=np.float32)) * rng.random((N, 8, 16, S), dtype=np.float32)).astype(np.int16)
        v = np.minimum(v, 255); return np.where(rng.random((N, 8, 1, S)) < 0.25, 255 - v, v)
    c = np.minimum((S * rng.random((N, 8, L)) ** 3).astype(np.int64), S - 1); c[:, ::2] = S - 1 - c[:, ::2]
    w = np.minimum(np.exp2(12.01 * rng.random((N, 8, 16, 2))).astype(np.int64) - (rng.random((N, 8, 16, 2)) < 0.05), 4095)
    k = np.maximum(np.minimum(np.exp2(12 * rng.random((N, 8, 16))).astype(np.int64) - 1, KM), 0)
    th = np.where(rng.random((N, 8)) < 0.25, rng.integers(0, 4081, (N, 8)), np.exp2(6 + 4 * rng.random((N, 8))).astype(np.int64))
    us = stones(); tp = stones()
    for q in range(N):
        g = int(rng.integers(0, 8))
        us[q, g] = rng.integers(0, 8, (16, S)); us[q, g, 0] += 248
        tp[q, g] = rng.integers(248, 256, (16, S)); tp[q, g, 8] = rng.integers(0, 2, S)
        w[q, g, :, 0] = 3072; w[q, g, 0, 0] = 4095; w[q, g, :, 1] = rng.integers(0, 4096, 16)
        k[q, g] = rng.permutation(KM + 1)[:16]; th[q, g] = 4080
    return pack(us, tp, c, w, k, th)
def setup_inputs_ties(rng):
    us, tp, c, w, k, th = parts(rng); flat = int(rng.integers(0, 8)); z = np.full((1, 16, 1), 255); z[0, 0] = 0
    for q in range(N):
        for g in range(8):
            pr = rng.integers(0, 256, (16, 12)); tp[q, g] = pr[:, rng.integers(0, 12, S)]
            us[q, g, :8] = pr[8:, rng.integers(0, 12, S)]; us[q, g, 8:] = pr[:8, rng.integers(0, 12, S)]
            th[q, g] = int(rng.choice(np.array([1, 400, 600, 700, 900])))
        us[q, flat] = 0; us[q, flat, 0] = 255; tp[q, flat] = 255; tp[q, flat, 8] = 0; th[q, flat] = 4080
        w[q, flat, 1, 0] ^= 1 - int(np.sum(w[q, flat, 1:, 0])) % 2
        if places(z, w[q, flat][None], k[q, flat][None])[0, 0, 0] == 0: k[q, flat, 0] ^= 1
    return pack(us, tp, c, w, k, th)
def check_inputs(d):
    bad = []
    for a, lo, hi in (("us", 0, 255), ("tp", 0, 255), ("c0", 0, S - 1), ("hw", 0, 4095), ("km", 0, KM), ("th", 0, 4080)):
        v = np.asarray(d[a]).astype(np.float64)
        if not (np.min(v) >= lo and np.max(v) <= hi): bad.append("range of " + a)
        elif np.any(v != np.floor(v)): bad.append("whole numbers in " + a)
    return bad
def reference(us, tp, c0, hw, km, th):
    U = np.zeros((N, 8, 16, W), np.int64); U[..., :S] = us.astype(np.float32).astype(np.int64).reshape(N, 8, 16, S)
    T = np.zeros((N, 8, 16, W), np.int64); T[..., :S] = tp.astype(np.float32).astype(np.int64).reshape(N, 8, 16, S)
    C = c0.astype(np.int64); w = hw.astype(np.int64).reshape(N, 8, 16, 2); k = km.astype(np.int64).reshape(N, 8, 16); t0 = th.astype(np.int64).reshape(N, 8)
    P = np.zeros(N, np.int64); out = []
    for t in range(RO):
        b = t0 + (P & 63)[:, None]; new, poor, zs = [], [], []
        for a in range(N):
            p, z = joined(C[a], T[a]); h, fit = probe(z, w[a], k[a], b[a], U[a]); win = lowest(h, fit)
            for g in range(8): U[a, g][:, h[g, win[g]]] = 255
            new.append(np.where(win, h, p)); poor.append(~fit); zs.append(z)
        for q in range(N):
            a = (q + 1 + t % (N - 1)) % N; sl = [np.flatnonzero(poor[q][g])[:CAP] for g in range(8)]
            z = np.zeros((8, 16, CAP), np.int64); use = np.zeros((8, CAP), bool)
            for g in range(8): z[g][:, :len(sl[g])] = zs[q][g][:, sl[g]]; use[g, :len(sl[g])] = True
            h, fit = probe(z, w[a], k[a], b[a], U[a]); win = lowest(h, fit & use)
            for g in range(8):
                s = np.flatnonzero(win[g]); n = h[g, s]; own = S + CAP * t + s
                U[q, g][:, own] = U[a, g][:, n]; T[q, g][:, own] = T[a, g][:, n]; U[a, g][:, n] = 255; new[q][g, sl[g][s]] = own
        P = np.array([int(np.sum(m)) for m in poor]); C = np.stack(new); out.append(C)
    return {"yc": np.concatenate(out, axis=2).astype(np.float32), "yu": U.reshape(N, 128, W).astype(np.float32).astype(BF)}

@@ -1,0 +1,561 @@
+from concourse.mybir import AluOpType as OP, ActivationFunctionType as AF
+
+RO, CAP, L, S = 5, 48, 256, 2048
+AREA = 560
+DL = S + 2 * AREA
+WID = DL + CAP
+ASKN = 800
+RETN = 104
+
+_sb = {
+    "U": (WID, "bfloat16"), "TW": (WID, "bfloat16"), "NW": (WID, "bfloat16"), "NH": (S, "bfloat16"),
+    "C0L": (16, "int32"), "HWI": (2, "int32"), "KMI": (1, "int32"), "THI": (1, "int32"),
+    "PIX": (1, "int32"), "PA_": (1, "int32"), "PG_": (1, "int32"), "COL": (16, "float32"), "SELC": (16, "float32"),
+    "GI": (128, "float32"), "YI": (144, "float32"), "AI": (256, "float32"),
+    "BO": (128, "bfloat16"), "BOH": (128, "float16"), "IDH": (128, "float16"), "SB": (144, "bfloat16"), "S16": (144, "bfloat16"), "SN": (144, "bfloat16"),
+    "S0": (144, "bfloat16"), "S256": (144, "bfloat16"), "SR": (2048, "bfloat16"), "PAM": (128, "bfloat16"), "PBM": (128, "bfloat16"),
+    "TRI": (128, "bfloat16"), "SHB": (128, "bfloat16"), "ONE": (128, "bfloat16"), "RST": (256, "float32"), "KEEP": (1024, "bfloat16"), "EA": (336, "float32"),
+    "MASK": (256, "bfloat16"), "DLP": (16, "float32"), "DLP32": (16, "float32"), "CL0": (16, "float32"),
+    "DC0": (16, "float32"), "DC1": (16, "float32"), "DC2": (16, "float32"), "DD0": (16, "float32"), "DD1": (16, "float32"),
+    "DD2": (16, "float32"), "FIXC": (16, "float32"), "FOUR": (16, "float32"),
+    "ZERO": (16, "float32"), "CI1": (256, "bfloat16"), "NB": (240, "bfloat16"), "C255": (256, "bfloat16"),
+    "S512": (48, "float32"), "E8": (128, "float32"), "THF": (16, "float32"), "TH16": (1, "float32"), "THR": (1, "float32"),
+    "WU": (16, "float16"), "WK": (128, "float16"), "WF": (2, "float32"), "WI": (2, "int32"), "KD": (16, "float16"), "KF": (1, "float32"),
+    "KI1": (1, "int32"), "KW": (16, "int32"), "KW2": (16, "int32"), "TMPC": (128, "float32"),
+    "ZB": (256, "bfloat16"), "UVI": (32, "int32"), "UVM": (32, "int32"), "TT": (16, "int32"), "TS2": (16, "int32"),
+    "TSF": (256, "float16"), "TXF": (256, "float16"), "HI": (256, "int32"), "HM": (256, "int32"), "H16": (256, "uint16"),
+    "ZS": (1536, "bfloat16"), "ZX": (4096, "bfloat16"), "DF": (4096, "bfloat16"), "KY": (256, "int32"),
+    "XN": (16, "bfloat16"), "SC": (16, "bfloat16"), "SX": (16, "float32"), "E2": (16, "float32"), "PT": (32, "float32"),
+    "PU": (32, "float32"), "APL": (16, "uint16"), "ASKW": (ASKN, "bfloat16"), "PIN": (1, "int32"), "PI2": (1, "int32"),
+    "MC": (16, "int32"), "P32": (16, "float32"), "NE": (16, "float32"), "CODE": (16, "bfloat16"), "OH": (256, "float16"), "HO": (256, "float16"),
+    "HR": (256, "float16"), "M1": (256, "float32"), "LS": (256, "float32"), "EI": (256, "bfloat16"), "EB": (1920, "bfloat16"),
+    "EL": (16, "float32"), "HD": (16, "float32"), "HMM": (16, "float32"), "CM": (256, "float32"), "CS": (256, "float32"), "WA": (16, "float32"),
+    "WM": (16, "float32"), "LAY": (16, "uint16"), "LEN": (4, "uint16"),
+    "CI": (16, "int32"), "CW": (16, "int32"), "CE": (16, "bfloat16"), "CFI": (16, "int32"), "CF2": (16, "float32"), "F1": (32, "bfloat16"),
+    "NN": (16, "bfloat16"), "NZ": (16, "float32"), "DZ": (16, "float32"), "PF": (16, "float32"), "JL": (16, "uint16"),
+    "J0": (ASKN, "bfloat16"), "JM": (256, "bfloat16"), "JF": (256, "bfloat16"), "SLOT": (16, "uint16"),
+    "F0R": (256, "float32"), "SLW": (ASKN, "float32"), "SLM": (48, "float32"), "SLS": (48, "float32"), "FIX": (4, "uint16"), "CF": (80, "float32"),
+    "ASKL": (RO * CAP, "bfloat16"), "RESP": (RETN, "bfloat16"), "RETL": (RO * RETN, "bfloat16"), "UB": (240, "bfloat16"),
+}
+_ps = ("pZ", "pUV", "pS", "pD", "pC", "pN", "pX", "pM")
+_place = {}
+_fill = {}
+for _k in _sb:
+    if _sb[_k][0] <= 48:
+        _d = _sb[_k][1]
+        _place[_k] = ("pack_" + _d, _fill.get(_d, 0))
+        _fill[_d] = _fill.get(_d, 0) + (_sb[_k][0] + 15) // 16 * 16
+SCRATCH = {k: ("sbuf", [128, _sb[k][0]], _sb[k][1]) for k in _sb if k not in _place}
+SCRATCH.update({"pack_" + k: ("sbuf", [128, _fill[k]], k) for k in _fill})
+SCRATCH.update({k: ("psum", [128, 512], "float32") for k in _ps})
+_bytes = {"bfloat16": 2, "float16": 2, "uint16": 2, "float32": 4, "int32": 4}
+SEMAPHORES = ["sV", "sA", "sP", "sG"] + ["d%d" % i for i in range(16)] + [a + str(t) for a in ("la", "lr", "aa", "ar") for t in range(RO)]
+CUTS = [(0, 64), (64, 96), (96, 160), (160, 208), (208, 240), (240, 256)]
+
+
+def rank_program(g, core, T, topo):
+    rank = T.rank_of(core)
+    if rank is None:
+        return
+    cores = list(T.cores)
+    N = len(cores)
+    Q = {"V": g.vector, "A": g.scalar, "P": g.tensor, "G": g, "S": g.sync}
+    count = {"sV": 0, "sA": 0, "sP": 0, "sG": 0}
+    know = {q: {} for q in Q}
+    snap = {}
+    hist = {}
+    ndma = [0]
+
+    def v(b, c0=0, c1=None, st=1, p=128, rows=None):
+        p = rows or p
+        if b in _place:
+            o = _place[b][1]
+            return (_place[b][0], o + c0, o + (_sb[b][0] if c1 is None else c1), st, p)
+        return (b, c0, (SCRATCH[b][1][1] if c1 is None else c1), st, p)
+
+    def ind(w, o):
+        return ("I", w, o)
+
+    def ap(x):
+        if x[0] == "I":
+            return ap(x[1]).indirect(ap(x[2]))
+        b, c0, c1, st, p = x
+        t = T[b]
+        if isinstance(p, tuple):
+            return t[p[0]:p[1]:p[2], c0:c1]
+        if st == 1:
+            return t[:, c0:c1] if p == 128 else t[0:p, c0:c1]
+        return t[:, c0:c1:st] if p == 128 else t[0:p, c0:c1:st]
+
+    def span(x):
+        n = _bytes[SCRATCH[x[0]][2]]
+        return x[0], x[1] * n // 16, (x[2] * n + 15) // 16
+
+    def learn(q, sem, val):
+        k = know[q]
+        if k.get(sem, 0) >= val:
+            return
+        k[sem] = val
+        for s2, v2 in snap.get((sem, val), {}).items():
+            if k.get(s2, 0) < v2:
+                k[s2] = v2
+
+    def need(q, rd, wr):
+        deps = {}
+        for x, w in [(x, False) for x in rd] + [(x, True) for x in wr]:
+            b, lo, hi = span(x)
+            ps = SCRATCH[b][0] == "psum"
+            keep = []
+            for e in hist.get(b, []):
+                elo, ehi, ew, eq, es, ev = e
+                hit = (ps and eq != q) or (not ps and elo < hi and lo < ehi)
+                if hit and (w or ew or ps):
+                    if deps.get(es, 0) < ev:
+                        deps[es] = ev
+                    if ps or (w and lo <= elo and ehi <= hi):
+                        continue
+                keep.append(e)
+            hist[b] = keep
+        for s in sorted(deps):
+            if know[q].get(s, 0) < deps[s]:
+                Q[q].wait_ge(T.sem[s], deps[s])
+                learn(q, s, deps[s])
+
+    def note(q, rd, wr, sem, val):
+        snap[(sem, val)] = dict(know[q])
+        for x, w in [(x, False) for x in rd] + [(x, True) for x in wr]:
+            b, lo, hi = span(x)
+            h = hist.setdefault(b, [])
+            h[:] = [e for e in h if not (e[0] == lo and e[1] == hi and e[2] == w and e[3] == q and e[4] == sem)]
+            h.append((lo, hi, w, q, sem, val))
+
+    def a_(x):
+        return ap(x) if isinstance(x, tuple) else x
+
+    def run(q, out, ins, f):
+        rd, wr = [], []
+        for x in ins:
+            if isinstance(x, tuple):
+                rd += [x[1], x[2]] if x[0] == "I" else [x]
+        if out[0] == "I":
+            wr.append(out[1])
+            rd.append(out[2])
+        else:
+            wr.append(out)
+        need(q, rd, wr)
+        s = "s" + q
+        count[s] += 1
+        f().then_inc(T.sem[s], 1)
+        note(q, rd, wr, s, count[s])
+
+    def cp(out, in_):
+        run("V", out, [in_], lambda: g.vector.tensor_copy(out=ap(out), in_=ap(in_)))
+
+    def tt(out, a, b, op):
+        run("V", out, [a, b], lambda: g.vector.tensor_tensor(out=ap(out), in0=ap(a), in1=ap(b), op=op))
+
+    def ts(out, a, s1, op0, s2=None, op1=None):
+        if op1 is None:
+            run("V", out, [a, s1], lambda: g.vector.tensor_scalar(out=ap(out), in0=ap(a), scalar1=a_(s1), scalar2=None, op0=op0))
+        else:
+            run("V", out, [a, s1, s2], lambda: g.vector.tensor_scalar(out=ap(out), in0=ap(a), scalar1=a_(s1), scalar2=a_(s2), op0=op0, op1=op1))
+
+    def scan(out, d0, d1, op0, op1):
+        run("V", out, [d0, d1], lambda: g.vector.tensor_tensor_scan(out=ap(out), data0=ap(d0), data1=ap(d1), initial=0.0, op0=op0, op1=op1))
+
+    def fill(out, c):
+        run("V", out, [], lambda: g.vector.memset(ap(out), c))
+
+    def act(out, in_, func=AF.Copy, scale=1.0, bias=0.0):
+        run("A", out, [in_, scale, bias], lambda: g.scalar.activation(out=ap(out), in_=ap(in_), func=func, bias=a_(bias), scale=a_(scale)))
+
+    def mm(out, lhsT, rhs, start=True, stop=True):
+        run("P", out, [lhsT, rhs], lambda: g.tensor.matmul(ap(out), ap(lhsT), ap(rhs), start=start, stop=stop))
+
+    def iota(out, pat, base=0, cm=0):
+        if SCRATCH[out[0]][2] != "int32":
+            run("G", out, [], lambda: g.iota(ap(out), pat, base, cm, allow_small_or_imprecise_dtypes=True))
+        else:
+            run("G", out, [], lambda: g.iota(ap(out), pat, base, cm))
+
+    def dma(q, out, in_):
+        rd = [in_] if isinstance(in_, tuple) else []
+        wr = [out] if isinstance(out, tuple) else []
+        need(q, rd, wr)
+        s = "d%d" % ndma[0]
+        ndma[0] += 1
+        Q[q].dma_start(out=a_(out), in_=a_(in_)).then_inc(T.sem[s], 16)
+        snap[(s, 16)] = dict(know[q])
+        for x, w in [(x, False) for x in rd] + [(x, True) for x in wr]:
+            b, lo, hi = span(x)
+            hist.setdefault(b, []).append((lo, hi, w, "dma", s, 16))
+
+    def engs(src, dst):
+        return topo.engines(src, dst)[:8]
+
+    def send(dst, out, in_, rsem, lsem):
+        need("G", [in_], [])
+        mask = 0
+        for e in engs(core, dst):
+            mask |= 1 << e
+        rid, pid = topo.addr(dst, core)
+        g.remote_dma(ap(out), ap(in_), T.sem[rsem], T.sem[lsem], pid, rid, mask)
+        b, lo, hi = span(in_)
+        hist.setdefault(b, []).append((lo, hi, False, "rdma", lsem, len(engs(core, dst))))
+        snap[(lsem, len(engs(core, dst)))] = dict(know["G"])
+
+    def arrives(x, src, rsem):
+        b, lo, hi = span(x)
+        hist.setdefault(b, []).append((lo, hi, True, "rdma", rsem, len(engs(src, core))))
+
+    dma("S", v("C0L"), T.c0[:])
+    dma("S", v("TW", 0, S), T.tp[:])
+    dma("A", v("HWI"), T.hw[:])
+    dma("A", v("KMI"), T.km[:])
+    dma("A", v("THI", p=8), T.th[:])
+    dma("A", v("U", 0, S), T.us[:])
+    iota(v("PIX"), [[0, 1]], 0, 1)
+    iota(v("GI"), [[1, 8], [0, 16]])
+    iota(v("AI"), [[0, 16], [1, 16]])
+    iota(v("YI"), [[1, 144]])
+    iota(v("CL0"), [[16, 16]])
+    iota(v("NW", 0, S), [[0, 128], [1, 16]])
+    iota(v("NH"), [[1, 128], [0, 16]])
+    dma("S", v("NW", 0, S, rows=(0, 128, 16)), v("NH", 0, S, rows=(0, 8, 1)))
+    iota(v("CI1"), [[1, 256]], 1)
+    iota(v("S512"), [[1, 48]], 256)
+    iota(v("NB"), [[0, 15], [1, 16]])
+    iota(v("NH", 0, 240), [[1, 15], [0, 16]], 128)
+    dma("S", v("NB", rows=(0, 128, 16)), v("NH", 0, 240, rows=(0, 8, 1)))
+    PIX, PA, PG = v("PIX"), v("PA_"), v("PG_")
+
+    def col(i):
+        return v("COL", i, i + 1)
+    ts(PA, PIX, 15, OP.bitwise_and)
+    ts(PG, PIX, 4, OP.arith_shift_right)
+    cp(col(0), PA)
+    cp(col(1), PG)
+    cp(col(3), PIX)
+    GI, YI = v("GI"), v("YI", 0, 128)
+    ts(v("BO"), GI, col(1), OP.is_equal)
+    ts(v("SELC"), v("AI", 0, 16), col(0), OP.is_equal)
+    for j in range(4):
+        act(v("KEEP", 256 * j, 256 * j + 256), v("AI"), AF.Sign)
+    act(v("ZS", 0, 1024), v("KEEP"), scale=0.0)
+    act(v("ZS", 1024, 1536), v("KEEP", 0, 512), scale=0.0)
+    ts(PA, PIX, 4, OP.arith_shift_right)
+    ts(PG, PA, 1, OP.bitwise_and)
+    cp(col(6), PG)
+    ts(col(5), col(6), -1.0, OP.mult, 1.0, OP.add)
+    cp(v("BOH"), v("BO"))
+    ts(col(7), col(0), 8.0, OP.is_ge)
+    ts(col(8), col(7), -1.0, OP.mult, 1.0, OP.add)
+    ts(col(9), col(3), -8.0, OP.add)
+    ts(col(10), col(3), 8.0, OP.add)
+    act(v("RST"), v("KEEP", 0, 256), scale=-1048577.0, bias=1048576.0)
+    ts(col(2), col(1), 16.0, OP.mult, 15.0, OP.add)
+    ts(v("SB"), v("YI"), col(2), OP.is_equal)
+    ts(col(11), col(0), 0.0, OP.is_equal)
+    ts(col(12), col(0), 1.0, OP.is_equal)
+    ts(col(13), col(11), 16.0, OP.mult)
+    tt(col(13), col(13), col(12), OP.add)
+    act(v("S16"), v("SB"), scale=16.0)
+    act(v("SN"), v("SB"), scale=col(13))
+    act(v("S0"), v("SB"), scale=col(11))
+    act(v("S256"), v("S0"), scale=256.0)
+    for r in range(16):
+        act(v("SR", 128 * r, 128 * r + 128), v("BO"), scale=v("SELC", r, r + 1))
+    cp(v("SX"), v("C0L"))
+
+    def flip(src, off, lst):
+        for h in (0, 1):
+            if off is None:
+                ts(v("PT", 16 * h, 16 * h + 16), src, col(5 + h), OP.mult)
+            else:
+                ts(v("PT", 16 * h, 16 * h + 16), src, off, OP.add, col(5 + h), OP.mult)
+        run("V", v("PU"), [v("PT")], lambda: g.vector.transpose(out=ap(v("PU")), in_=ap(v("PT"))))
+        tt(lst, v("PU", 0, 16), v("PU", 16, 32), OP.add)
+    flip(v("SX"), None, v("JL"))
+    ts(v("PAM"), YI, col(9), OP.is_equal, col(7), OP.mult)
+    ts(v("PBM"), YI, col(10), OP.is_equal, col(8), OP.mult)
+    ts(v("WI"), v("HWI"), 2047, OP.bitwise_and)
+    cp(v("WF"), v("WI"))
+    for i in (0, 1):
+        ts(v("WU", 8 * i, 8 * i + 8), v("GI", 0, 128, 16), col(1), OP.is_equal, v("WF", i, i + 1), OP.mult)
+    ts(v("KI1"), v("KMI"), 2047, OP.bitwise_and)
+    cp(v("KF"), v("KI1"))
+    ts(v("KD"), v("AI", 0, 16), col(0), OP.is_equal, v("KF"), OP.mult)
+    mm(v("pX", 0, 16), v("BOH"), v("KD"))
+    ts(v("KW"), v("pX", 0, 16), v("WF", 0, 1), OP.mult)
+    ts(v("KW2"), v("KW"), 2047, OP.bitwise_and)
+    for j in range(8):
+        tt(v("WK", 16 * j, 16 * j + 16), v("KW2"), v("BO", 16 * j, 16 * j + 16), OP.mult)
+    ts(v("IDH"), YI, col(3), OP.is_equal)
+    ts(v("TSF"), v("AI"), 0.0, OP.mult)
+    A0 = S
+    cp(v("TW", A0, A0 + L), ind(v("TW", 0, S), v("JL")))
+
+    def sel(b, r):
+        return v(b, 15 - r, 143 - r)
+
+    def srow(r):
+        return v("SR", 128 * r, 128 * r + 128)
+
+    def setup_b():
+        act(v("NW", A0, A0 + L), ind(v("NW", 0, S), v("JL")))
+        act(v("NW", A0 + L, WID), v("KEEP", 0, WID - A0 - L), scale=0.0)
+        act(v("TW", A0 + L, WID), v("KEEP", 0, WID - A0 - L), scale=0.0)
+        fill(v("U", S, WID), 0.0)
+
+    def setup_c():
+        cp(v("THF", 0, 1, p=8), v("THI", p=8))
+        ts(v("E8", p=8), v("GI", p=8), v("COL", 3, 4, p=8), OP.is_equal)
+        mm(v("pX", 16, 17), v("E8", p=8), v("THF", 0, 1, p=8))
+        ts(v("TH16"), v("pX", 16, 17), 16.0, OP.mult, -15.0, OP.add)
+        cp(v("THR"), v("TH16"))
+        ts(v("TMPC"), v("AI", 0, 128), col(0), OP.is_gt)
+        tt(v("TRI"), v("TMPC"), v("BO"), OP.mult)
+        ts(col(15), col(3), 1.0, OP.add)
+        ts(col(4), col(0), 15.0, OP.is_lt)
+        ts(v("SHB"), YI, col(15), OP.is_equal, col(4), OP.mult)
+        ts(col(14), col(0), 16.0, OP.mult)
+        ts(v("DLP"), v("AI", 0, 16), col(14), OP.add, 272.0, OP.add)
+        ts(v("DLP32"), v("DLP"), 0.03125, OP.mult)
+        ts(v("FIXC"), v("DLP"), 272.0 + 254.0, OP.is_ge, 8.0, OP.mult)
+        fill(v("FOUR"), 4.0)
+        fill(v("ZERO"), 0.0)
+
+    def setup_d():
+        ts(v("MASK"), v("AI"), col(0), OP.is_equal)
+        ts(PA, PIX, 1, OP.add)
+        ts(PG, PA, 15, OP.bitwise_and)
+        cp(col(4), PG)
+        ts(v("DC0"), v("CL0"), col(0), OP.add, float(S), OP.add)
+        ts(v("DC1"), v("DC0"), float(AREA), OP.add)
+        ts(v("DC2"), v("DC0"), float(DL - S), OP.add)
+        for i in "012":
+            ts(v("DD" + i), v("DC" + i), 1.0, OP.add)
+        fill(v("C255"), 255.0)
+        fill(v("ONE"), 1.0)
+        fill(v("RESP"), 0.0)
+
+    def hash_a(z, zc, n):
+        m = min(n, 128)
+        nb = (n + 127) // 128
+        for b in range(nb):
+            for i in (0, 1):
+                mm(v("pUV", 16 * i + 8 * b, 16 * i + 8 * b + 8, p=m), v(z, zc + 128 * b, zc + 128 * b + m), v("WU", 8 * i, 8 * i + 8))
+        mm(v("pS", 0, n), v("WK"), v(z, zc, zc + n), True, False)
+        cp(v("UVI", p=m), v("pUV", 0, 32, p=m))
+        ts(v("UVM", p=m), v("UVI", p=m), 2047, OP.bitwise_and)
+        tt(v("TT", p=m), v("UVM", 0, 16, p=m), v("UVM", 16, 32, p=m), OP.mult)
+        ts(v("TS2", p=m), v("TT", p=m), 5, OP.arith_shift_right, 2047, OP.bitwise_and)
+        k = 8 * nb
+        cp(v("TSF", 0, 16 * k, 16, p=m), v("TS2", 0, k, p=m))
+        scan(v("TXF", 0, 16 * k, p=m), v("KEEP", 0, 16 * k, p=m), v("TSF", 0, 16 * k, p=m), OP.mult, OP.add)
+        for b in range(nb):
+            mm(v("pS", 128 * b, 128 * b + m), v("TXF", 128 * b, 128 * b + 128, p=m), v("IDH", 0, m, p=m), False, b == nb - 1)
+
+    def hash_b(n):
+        cp(v("HI", 0, n), v("pS", 0, n))
+        ts(v("HM", 0, n), v("HI", 0, n), 2047, OP.bitwise_and)
+        cp(v("H16", 0, n), v("HM", 0, n))
+
+    def expand(k0, k1):
+        scan(v("ZX", 16 * k0, 16 * k1), v("KEEP", 0, 16 * (k1 - k0)), v("ZS", 16 * k0, 16 * k1), OP.mult, OP.add)
+
+    def dist(cuts, n, hooks):
+        for i, (k0, k1) in enumerate(cuts):
+            x = v("DF", 16 * k0, 16 * k1)
+            tt(x, ind(v("U", 0, S), v("H16", k0, k1)), v("ZX", 16 * k0, 16 * k1), OP.subtract)
+            act(x, x, AF.Abs)
+            for h in hooks.get(i, ()):
+                h()
+            for r in range(k0 // 16, k1 // 16):
+                mm(v("pD", 0, 256), sel("S16", r), v("DF", 256 * r, 256 * r + 256), r == 0, r == n // 16 - 1)
+        for h in hooks.get("tail", ()):
+            h()
+        scan(v("KY"), v("RST"), v("pD", 0, 256), OP.add, OP.min)
+
+    KEY = v("KY", 15, 256, 16)
+
+    def choose(n, own, dc, lst, hook):
+        k = n // 16
+        ts(v("P32"), KEY, v("THR"), OP.is_ge, 32.0, OP.mult)
+        ts(v("MC"), KEY, 15, OP.bitwise_and)
+        if own:
+            tt(v("NE"), v("P32"), v("NZ"), OP.max)
+        tt(v("CODE"), v("NE") if own else v("P32"), v("MC"), OP.add)
+        for r in range(k):
+            mm(v("pC", 16 * r, 16 * r + 16), srow(r), v("CODE"))
+        hook()
+        ts(v("OH", 0, n), v("pC", 0, n), col(4), OP.is_equal)
+        tt(v("HO", 0, n), v("OH", 0, n), v("HM", 0, n), OP.mult)
+        h1 = v("pC", 256, 256 + n)
+        mm(h1, v("BOH"), v("OH", 0, n), True, False)
+        mm(h1, v("BOH"), v("HO", 0, n), False, True)
+        tt(v("M1", 0, n), h1, v("MASK", 0, n), OP.mult)
+        cp(v("HR", 0, n), h1)
+        scan(v("LS", 0, n), v("KEEP", 0, n), v("M1", 0, n), OP.mult, OP.add)
+        tt(v("EI", 0, n), h1, v("LS", 0, n), OP.is_equal)
+        mm(v("pN", 0, n), v("BO"), v("EI", 0, n), True, k == 1)
+        kv = 11 if own else k - 1
+        o = [0]
+        for c in range(k - 1):
+            o.append(o[c] + n - 16 * (c + 1))
+        for c in range(kv, k - 1):
+            act(v("EA", o[c] - o[kv], o[c + 1] - o[kv]), v("pC", 256 + 16 * (c + 1), 256 + n), AF.Abs, -1.0, v("LS", 16 * c + 15, 16 * c + 16))
+        if kv < k - 1:
+            act(v("EB", o[kv], o[k - 1]), v("EA", 0, o[k - 1] - o[kv]), AF.Relu, -1.0, 1.0)
+        for c in range(k - 1):
+            if c < kv:
+                ts(v("EB", o[c], o[c + 1]), v("HR", 16 * (c + 1), n), v("LS", 16 * c + 15, 16 * c + 16), OP.is_equal)
+            mm(v("pN", 16 * (c + 1), n), v("BO"), v("EB", o[c], o[c + 1]), False, c == k - 2)
+        HL = v("LS", 15, n, 16)
+        ts(v("EL", 0, k), HL, 0.0, OP.is_gt)
+        tt(v("HD", 0, k), HL, v("DD" + dc[2], 0, k), OP.subtract)
+        tt(v("HMM", 0, k), v("HD", 0, k), v("EL", 0, k), OP.mult)
+        tt(v("CM", 0, n), v("pN", 0, n), v("MASK", 0, n), OP.mult)
+        scan(v("CS", 0, n), v("KEEP", 0, n), v("CM", 0, n), OP.mult, OP.add)
+        ts(v("WA", 0, k), v("CS", 15, n, 16), 1.0, OP.is_equal)
+        tt(v("WM", 0, k), v("WA", 0, k), v("HMM", 0, k), OP.mult)
+        tt(v(lst, 0, k), v("WM", 0, k), v(dc, 0, k), OP.add)
+
+    def numbers(A):
+        for r in range(16):
+            mm(v("pM", 272, 288), sel("SN", r), v("NW", A + 16 * r, A + 16 * r + 16), r == 0, r == 15)
+
+    def put_course(t):
+        cp(v("CF", 16 * t, 16 * t + 16), v("CI"))
+        dma("S", T.yc[:, 256 * t:256 * t + 256], v("CF", 16 * t, 16 * t + 16))
+
+    def widths():
+        cp(v("CI"), v("pM", 272, 288))
+        ts(v("CW"), v("CI"), 3, OP.bitwise_and)
+        scan(v("CE"), v("CW"), v("FOUR"), OP.add, OP.add)
+        mm(v("pX", 16, 17), v("TRI"), v("CE", 15, 16))
+        ts(v("CFI"), v("CE"), v("pX", 16, 17), OP.add, 0.2, OP.mult)
+        ts(v("CF2"), v("CFI"), 256.0, OP.min, 0.03125, OP.mult)
+        tt(v("F1", 1, 17), v("CF2"), v("FIXC"), OP.max)
+        mm(v("pX", 17, 18), v("SHB"), v("F1", 16, 17))
+        cp(v("F1", 0, 1), v("pX", 17, 18))
+        tt(v("NN"), v("F1", 1, 17), v("F1", 0, 16), OP.subtract)
+        ts(v("NZ"), v("NN"), 0.0, OP.is_equal, 32.0, OP.mult)
+
+    def slots_a():
+        for r in range(16):
+            mm(v("pM", 16 * r, 16 * r + 16), srow(r), v("F1", 0, 16))
+        act(v("F0R"), v("pM", 0, 256), scale=32.0)
+        fill(v("J0", 0, 256), 0.0)
+        cp(v("SLW", 0, CAP), v("S512"))
+        tt(v("DZ"), v("NZ"), v("DLP32"), OP.mult)
+        ts(v("PF"), v("F1", 0, 16), 32.0, OP.mult)
+        tt(v("PF"), v("DZ"), v("PF"), OP.add)
+        flip(v("PF"), None, v("JL"))
+
+    def slots_b():
+        cp(ind(v("J0"), v("JL")), v("CI1"))
+        scan(v("JM"), v("J0", 0, 256), v("J0", 0, 256), OP.max, OP.max)
+        act(v("JF"), v("J0", 0, 256), AF.Sign)
+
+    def slots_m():
+        for b, x in (("S0", "JM"), ("S256", "JF")):
+            for p in range(16):
+                mm(v("pM", 256, 272), sel(b, p), v(x, p, 256, 16), b == "S0" and p == 0, b == "S256" and p == 15)
+
+    def slots_c():
+        cp(ind(v("SLW"), v("APL")), v("F0R"))
+        tt(v("SLM"), v("SLW", 0, CAP), v("MASK", 0, CAP), OP.mult)
+        scan(v("SLS"), v("KEEP", 0, CAP), v("SLM"), OP.mult, OP.add)
+
+    for t in range(RO):
+        A = S + AREA * (t % 2)
+        B = S + AREA * (1 - t % 2)
+        lender = cores[(rank + 1 + t % (N - 1)) % N]
+        asker = cores[(rank - 1 - t % (N - 1)) % N]
+        mm(v("pZ", 0, 256), v("PAM"), v("TW", A, A + L), True, False)
+        mm(v("pZ", 0, 255), v("PBM"), v("TW", A + 1, A + L), False, True)
+        cp(v("ZB"), v("pZ", 0, 256))
+        for m in range(16):
+            act(v("ZX", 1536 + m, 4096, 16), v("ZB", 96, 256))
+        cp(v("ZS", 0, 1536, 16), v("ZB", 0, 96))
+        hash_a("ZB", 0, 256)
+        if t == 0:
+            setup_b()
+        else:
+            cp(ind(v("NW", A, A + AREA), v("FIX", 0, 3)), v("NB", CAP * (t - 1), CAP * t))
+            numbers(A)
+        expand(0, 64)
+        hash_b(256)
+
+        def course():
+            expand(64, 96)
+            if t == 0:
+                setup_c()
+                numbers(A)
+            widths()
+            if t:
+                put_course(t - 1)
+            fill(v("ASKW", 0, CAP), 1024.0)
+        dist(CUTS, 256, {0: [course], "tail": [setup_d] * (t == 0) + [slots_a]})
+
+        def ask():
+            tt(v("XN"), v("P32"), v("NN"), OP.mult)
+            scan(v("SC"), v("XN"), v("ZERO"), OP.add, OP.add)
+            mm(v("pX", 16, 17), v("TRI"), v("SC", 15, 16))
+            ts(v("E2"), v("XN"), 0.0, OP.is_equal)
+            tt(v("E2"), v("E2"), v("DLP"), OP.mult)
+            tt(v("SX"), v("SC"), v("XN"), OP.subtract)
+            tt(v("SX"), v("SX"), v("E2"), OP.add)
+            flip(v("SX"), v("pX", 16, 17), v("APL"))
+            cp(ind(v("ASKW"), v("APL")), v("ZB"))
+            send(lender, v("ASKL", CAP * t, CAP * t + CAP), v("ASKW", 0, CAP), "aa%d" % t, "la%d" % t)
+            arrives(v("ASKL", CAP * t, CAP * t + CAP), asker, "aa%d" % t)
+        choose(256, True, "DC%d" % (t % 2), "LAY", ask)
+        cp(ind(v("U", 0, DL), v("LAY")), v("C255"))
+        act(v("TW", A + L, A + 2 * L), ind(v("TW", 0, A + L), v("LAY")))
+        act(v("NW", A + L, A + 2 * L), ind(v("NW", 0, A + L), v("LAY")))
+        z = CAP * t
+        hash_a("ASKL", z, CAP)
+        cp(v("ZS", 0, 16 * CAP, 16), v("ASKL", z, z + CAP))
+        expand(0, CAP)
+        hash_b(CAP)
+        dist([(0, 32), (32, 48)], CAP, {"tail": [slots_b]})
+        choose(CAP, False, "DC2", "LEN", lambda: None)
+        slots_m()
+        act(v("RESP", 48, 96), ind(v("TW"), v("LEN", 0, 3)))
+        cp(v("RESP", 0, 48), ind(v("U"), v("LEN", 0, 3)))
+        ts(v("RESP", 96, 99), v("LEN", 0, 3), float(DL), OP.is_ge, 256.0, OP.mult)
+        send(asker, v("RETL", RETN * t, RETN * t + RETN), v("RESP"), "ar%d" % t, "lr%d" % t)
+        arrives(v("RETL", RETN * t, RETN * t + RETN), lender, "ar%d" % t)
+        slots_c()
+        ts(v("SLOT"), v("pM", 256, 272), -1.0, OP.add)
+        cp(ind(v("U"), v("LEN", 0, 3)), v("C255", 0, 48))
+        fill(v("U", DL, WID), 0.0)
+        act(v("TW", B, B + L), ind(v("TW", A, A + 2 * L), v("SLOT")))
+        act(v("NW", B, B + L), ind(v("NW", A, A + 2 * L), v("SLOT")))
+        mm(v("pX", 18, 19), v("ONE"), v("SC", 15, 16))
+        cp(v("PIN"), v("pX", 18, 19))
+        ts(v("PI2"), v("PIN"), 63, OP.bitwise_and)
+        ts(v("THR"), v("PI2"), 16.0, OP.mult, v("TH16"), OP.add)
+        r0 = RETN * t
+        tt(v("FIX", 0, 3), v("SLS", 15, CAP, 16), v("RETL", r0 + 96, r0 + 99), OP.add)
+        if t < RO - 1:
+            cp(ind(v("TW", B, B + AREA), v("FIX", 0, 3)), v("RETL", r0 + 48, r0 + 96))
+        act(v("UB", CAP * t, CAP * t + CAP), v("RETL", r0, r0 + 48))
+    dma("S", T.yu[:, 0:S], v("U", 0, S))
+    B = S + AREA * (RO % 2)
+    cp(ind(v("NW", B, B + AREA), v("FIX", 0, 3)), v("NB", CAP * (RO - 1), CAP * RO))
+    numbers(B)
+    cp(v("CI"), v("pM", 272, 288))
+    put_course(RO - 1)
+    dma("S", T.yu[:, S:S + RO * CAP], v("UB"))
+    for s in ("sV", "sA", "sP", "sG"):
+        g.wait_ge(T.sem[s], count[s])
+    for i in range(ndma[0]):
+        g.sync.wait_ge(T.sem["d%d" % i], 16)
+    for t in range(RO):
+        lender = cores[(rank + 1 + t % (N - 1)) % N]
+        asker = cores[(rank - 1 - t % (N - 1)) % N]
+        for s, n in (("la", len(engs(core, lender))), ("lr", len(engs(core, asker))), ("aa", len(engs(asker, core))), ("ar", len(engs(lender, core)))):
+            g.wait_ge(T.sem[s + str(t)], n)

@@ -22,16 +22,16 @@ _sb = {
     "S512": (48, "float32"), "E8": (128, "float32"), "THF": (16, "float32"), "TH16": (1, "float32"), "THR": (1, "float32"),
     "WU": (16, "float16"), "WK": (128, "float16"), "WF": (2, "float32"), "WI": (2, "int32"), "KD": (16, "float16"), "KF": (1, "float32"),
     "KI1": (1, "int32"), "KW": (16, "int32"), "KW2": (16, "int32"), "TMPC": (128, "float32"),
-    "ZB": (256, "bfloat16"), "UVI": (32, "int32"), "UVM": (32, "int32"), "TT": (16, "int32"), "TS2": (16, "int32"),
-    "TSF": (256, "float16"), "TXF": (256, "float16"), "HI": (256, "int32"), "HM": (256, "int32"), "H16": (256, "uint16"),
+    "ZB": (256, "bfloat16"), "UVI": (32, "int32"), "UVM": (32, "int32"), "TT": (16, "int32"), "TSI": (256, "int32"),
+    "BO300": (128, "float16"), "TXF": (256, "float16"), "HI": (256, "int32"), "HM": (256, "int32"), "H16": (256, "uint16"),
     "ZS": (1536, "bfloat16"), "ZX": (4096, "bfloat16"), "DF": (4096, "bfloat16"), "KY": (256, "int32"),
-    "XN": (16, "bfloat16"), "SC": (16, "bfloat16"), "SX": (16, "float32"), "E2": (16, "float32"), "PT": (32, "float32"),
+    "PQ": (16, "float32"), "XN": (16, "bfloat16"), "SC": (32, "bfloat16"), "SX": (16, "float32"), "E2": (16, "float32"), "PT": (32, "float32"),
     "PU": (32, "float32"), "APL": (16, "uint16"), "ASKW": (ASKN, "bfloat16"), "PIN": (1, "int32"), "PI2": (1, "int32"),
     "MC": (16, "int32"), "P32": (16, "float32"), "NE": (16, "float32"), "CODE": (16, "bfloat16"), "OH": (256, "float16"), "HO": (256, "float16"),
     "HR": (256, "float16"), "M1": (256, "float32"), "LS": (256, "float32"), "EI": (256, "bfloat16"), "EB": (1920, "bfloat16"),
     "EL": (16, "float32"), "HD": (16, "float32"), "HMM": (16, "float32"), "CM": (256, "float32"), "CS": (256, "float32"), "WA": (16, "float32"),
     "WM": (16, "float32"), "LAY": (16, "uint16"), "LEN": (4, "uint16"),
-    "CI": (16, "int32"), "CW": (16, "int32"), "CE": (16, "bfloat16"), "CFI": (16, "int32"), "CF2": (16, "float32"), "F1": (32, "bfloat16"),
+    "CI": (16, "int32"), "CW": (16, "int32"), "CE": (32, "bfloat16"), "CFI": (32, "int32"), "F1": (32, "bfloat16"),
     "NN": (16, "bfloat16"), "NZ": (16, "float32"), "DZ": (16, "float32"), "PF": (16, "float32"), "JL": (16, "uint16"),
     "J0": (ASKN, "bfloat16"), "JM": (256, "bfloat16"), "JF": (256, "bfloat16"), "SLOT": (16, "uint16"),
     "F0R": (256, "float32"), "SLW": (ASKN, "float32"), "SLM": (48, "float32"), "SLS": (48, "float32"), "FIX": (4, "uint16"), "CF": (80, "float32"),
@@ -252,14 +252,14 @@ def rank_program(g, core, T, topo):
     ts(col(8), col(7), -1.0, OP.mult, 1.0, OP.add)
     ts(col(9), col(3), -8.0, OP.add)
     ts(col(10), col(3), 8.0, OP.add)
-    act(v("RST"), v("KEEP", 0, 256), scale=-1048577.0, bias=1048576.0)
+    act(v("RST"), v("KEEP", 0, 256), scale=-1048578.0, bias=1048576.0)
     ts(col(2), col(1), 16.0, OP.mult, 15.0, OP.add)
     ts(v("SB"), v("YI"), col(2), OP.is_equal)
     ts(col(11), col(0), 0.0, OP.is_equal)
     ts(col(12), col(0), 1.0, OP.is_equal)
     ts(col(13), col(11), 16.0, OP.mult)
     tt(col(13), col(13), col(12), OP.add)
-    act(v("S16"), v("SB"), scale=16.0)
+    act(v("S16"), v("SB"), scale=32.0)
     act(v("SN"), v("SB"), scale=col(13))
     act(v("S0"), v("SB"), scale=col(11))
     act(v("S256"), v("S0"), scale=256.0)
@@ -291,7 +291,7 @@ def rank_program(g, core, T, topo):
     for j in range(8):
         tt(v("WK", 16 * j, 16 * j + 16), v("KW2"), v("BO", 16 * j, 16 * j + 16), OP.mult)
     ts(v("IDH"), YI, col(3), OP.is_equal)
-    ts(v("TSF"), v("AI"), 0.0, OP.mult)
+    ts(v("TSI"), v("AI"), 0.0, OP.mult)
     A0 = S
     cp(v("TW", A0, A0 + L), ind(v("TW", 0, S), v("JL")))
 
@@ -305,31 +305,36 @@ def rank_program(g, core, T, topo):
         act(v("NW", A0, A0 + L), ind(v("NW", 0, S), v("JL")))
         act(v("NW", A0 + L, WID), v("KEEP", 0, WID - A0 - L), scale=0.0)
         act(v("TW", A0 + L, WID), v("KEEP", 0, WID - A0 - L), scale=0.0)
+        prefill()
         fill(v("U", S, WID), 0.0)
+
+    def prefill():
+        act(v("ASKW", 0, CAP), v("KEEP", 0, CAP), scale=0.0, bias=1024.0)
+        act(v("SLW", 0, CAP), v("S512"))
+        act(v("J0", 0, 256), v("KEEP", 0, 256), scale=0.0)
 
     def setup_c():
         cp(v("THF", 0, 1, p=8), v("THI", p=8))
         ts(v("E8", p=8), v("GI", p=8), v("COL", 3, 4, p=8), OP.is_equal)
         mm(v("pX", 16, 17), v("E8", p=8), v("THF", 0, 1, p=8))
-        ts(v("TH16"), v("pX", 16, 17), 16.0, OP.mult, -15.0, OP.add)
+        ts(v("TH16"), v("pX", 16, 17), 32.0, OP.mult, -30.0, OP.add)
         cp(v("THR"), v("TH16"))
         ts(v("TMPC"), v("AI", 0, 128), col(0), OP.is_gt)
         tt(v("TRI"), v("TMPC"), v("BO"), OP.mult)
-        ts(col(15), col(3), 1.0, OP.add)
-        ts(col(4), col(0), 15.0, OP.is_lt)
-        ts(v("SHB"), YI, col(15), OP.is_equal, col(4), OP.mult)
         ts(col(14), col(0), 16.0, OP.mult)
         ts(v("DLP"), v("AI", 0, 16), col(14), OP.add, 272.0, OP.add)
-        ts(v("DLP32"), v("DLP"), 0.03125, OP.mult)
-        ts(v("FIXC"), v("DLP"), 272.0 + 254.0, OP.is_ge, 8.0, OP.mult)
-        fill(v("FOUR"), 4.0)
+        ts(v("FOUR"), v("DLP"), 272.0 + 254.0, OP.is_equal, 1600.0, OP.mult)
+        ts(v("FOUR"), v("FOUR"), 4.0, OP.add)
         fill(v("ZERO"), 0.0)
+        fill(v("CE", 0, 1), 0.0)
+        fill(v("SC", 0, 1), 0.0)
 
     def setup_d():
         ts(v("MASK"), v("AI"), col(0), OP.is_equal)
         ts(PA, PIX, 1, OP.add)
         ts(PG, PA, 15, OP.bitwise_and)
-        cp(col(4), PG)
+        ts(col(4), PG, 2.0, OP.mult)
+        ts(v("BO300"), v("BO"), 300.0, OP.mult)
         ts(v("DC0"), v("CL0"), col(0), OP.add, float(S), OP.add)
         ts(v("DC1"), v("DC0"), float(AREA), OP.add)
         ts(v("DC2"), v("DC0"), float(DL - S), OP.add)
@@ -349,10 +354,9 @@ def rank_program(g, core, T, topo):
         cp(v("UVI", p=m), v("pUV", 0, 32, p=m))
         ts(v("UVM", p=m), v("UVI", p=m), 2047, OP.bitwise_and)
         tt(v("TT", p=m), v("UVM", 0, 16, p=m), v("UVM", 16, 32, p=m), OP.mult)
-        ts(v("TS2", p=m), v("TT", p=m), 5, OP.arith_shift_right, 2047, OP.bitwise_and)
         k = 8 * nb
-        cp(v("TSF", 0, 16 * k, 16, p=m), v("TS2", 0, k, p=m))
-        scan(v("TXF", 0, 16 * k, p=m), v("KEEP", 0, 16 * k, p=m), v("TSF", 0, 16 * k, p=m), OP.mult, OP.add)
+        ts(v("TSI", 0, 16 * k, 16, p=m), v("TT", 0, k, p=m), 5, OP.arith_shift_right, 2047, OP.bitwise_and)
+        scan(v("TXF", 0, 16 * k, p=m), v("KEEP", 0, 16 * k, p=m), v("TSI", 0, 16 * k, p=m), OP.mult, OP.add)
         for b in range(nb):
             mm(v("pS", 128 * b, 128 * b + m), v("TXF", 128 * b, 128 * b + 128, p=m), v("IDH", 0, m, p=m), False, b == nb - 1)
 
@@ -381,11 +385,15 @@ def rank_program(g, core, T, topo):
 
     def choose(n, own, dc, lst, hook):
         k = n // 16
-        ts(v("P32"), KEY, v("THR"), OP.is_ge, 32.0, OP.mult)
-        ts(v("MC"), KEY, 15, OP.bitwise_and)
+        ts(v("PQ"), KEY, v("THR"), OP.is_ge)
         if own:
-            tt(v("NE"), v("P32"), v("NZ"), OP.max)
-        tt(v("CODE"), v("NE") if own else v("P32"), v("MC"), OP.add)
+            tt(v("XN"), v("PQ"), v("NN"), OP.mult)
+            scan(v("SC", 1, 17), v("XN"), v("ZERO"), OP.add, OP.add)
+            mm(v("pX", 16, 17), v("TRI"), v("SC", 16, 17))
+        ts(v("MC"), KEY, 30, OP.bitwise_and)
+        if own:
+            tt(v("NE"), v("PQ"), v("NZ"), OP.max)
+        tt(v("CODE"), v("NE") if own else v("PQ"), v("MC"), OP.add)
         for r in range(k):
             mm(v("pC", 16 * r, 16 * r + 16), srow(r), v("CODE"))
         hook()
@@ -394,11 +402,12 @@ def rank_program(g, core, T, topo):
         h1 = v("pC", 256, 256 + n)
         mm(h1, v("BOH"), v("OH", 0, n), True, False)
         mm(h1, v("BOH"), v("HO", 0, n), False, True)
+        mm(v("pN", 0, n), v("BO300"), v("OH", 0, n), True, False)
         tt(v("M1", 0, n), h1, v("MASK", 0, n), OP.mult)
         cp(v("HR", 0, n), h1)
         scan(v("LS", 0, n), v("KEEP", 0, n), v("M1", 0, n), OP.mult, OP.add)
         tt(v("EI", 0, n), h1, v("LS", 0, n), OP.is_equal)
-        mm(v("pN", 0, n), v("BO"), v("EI", 0, n), True, k == 1)
+        mm(v("pN", 0, n), v("BO"), v("EI", 0, n), False, False)
         kv = 11 if own else k - 1
         o = [0]
         for c in range(k - 1):
@@ -412,13 +421,11 @@ def rank_program(g, core, T, topo):
                 ts(v("EB", o[c], o[c + 1]), v("HR", 16 * (c + 1), n), v("LS", 16 * c + 15, 16 * c + 16), OP.is_equal)
             mm(v("pN", 16 * (c + 1), n), v("BO"), v("EB", o[c], o[c + 1]), False, c == k - 2)
         HL = v("LS", 15, n, 16)
-        ts(v("EL", 0, k), HL, 0.0, OP.is_gt)
         tt(v("HD", 0, k), HL, v("DD" + dc[2], 0, k), OP.subtract)
-        tt(v("HMM", 0, k), v("HD", 0, k), v("EL", 0, k), OP.mult)
         tt(v("CM", 0, n), v("pN", 0, n), v("MASK", 0, n), OP.mult)
         scan(v("CS", 0, n), v("KEEP", 0, n), v("CM", 0, n), OP.mult, OP.add)
-        ts(v("WA", 0, k), v("CS", 15, n, 16), 1.0, OP.is_equal)
-        tt(v("WM", 0, k), v("WA", 0, k), v("HMM", 0, k), OP.mult)
+        ts(v("WA", 0, k), v("CS", 15, n, 16), 301.0, OP.is_equal)
+        tt(v("WM", 0, k), v("WA", 0, k), v("HD", 0, k), OP.mult)
         tt(v(lst, 0, k), v("WM", 0, k), v(dc, 0, k), OP.add)
 
     def numbers(A):
@@ -426,31 +433,26 @@ def rank_program(g, core, T, topo):
             mm(v("pM", 272, 288), sel("SN", r), v("NW", A + 16 * r, A + 16 * r + 16), r == 0, r == 15)
 
     def put_course(t):
-        cp(v("CF", 16 * t, 16 * t + 16), v("CI"))
+        act(v("CF", 16 * t, 16 * t + 16), v("pM", 272, 288))
         dma("S", T.yc[:, 256 * t:256 * t + 256], v("CF", 16 * t, 16 * t + 16))
 
-    def widths():
-        cp(v("CI"), v("pM", 272, 288))
-        ts(v("CW"), v("CI"), 3, OP.bitwise_and)
-        scan(v("CE"), v("CW"), v("FOUR"), OP.add, OP.add)
-        mm(v("pX", 16, 17), v("TRI"), v("CE", 15, 16))
-        ts(v("CFI"), v("CE"), v("pX", 16, 17), OP.add, 0.2, OP.mult)
-        ts(v("CF2"), v("CFI"), 256.0, OP.min, 0.03125, OP.mult)
-        tt(v("F1", 1, 17), v("CF2"), v("FIXC"), OP.max)
-        mm(v("pX", 17, 18), v("SHB"), v("F1", 16, 17))
-        cp(v("F1", 0, 1), v("pX", 17, 18))
+    def widths(t):
+        if t:
+            cp(v("CI"), v("pM", 272, 288))
+        ts(v("CW"), v("CI") if t else v("C0L"), 3, OP.bitwise_and)
+        scan(v("CE", 1, 17), v("CW"), v("FOUR"), OP.add, OP.add)
+        mm(v("pX", 16, 17), v("TRI"), v("CE", 16, 17))
+        ts(v("CFI", 0, 17), v("CE", 0, 17), v("pX", 16, 17), OP.add, 0.2, OP.mult)
+        ts(v("F1", 0, 17), v("CFI", 0, 17), 256.0, OP.min)
         tt(v("NN"), v("F1", 1, 17), v("F1", 0, 16), OP.subtract)
-        ts(v("NZ"), v("NN"), 0.0, OP.is_equal, 32.0, OP.mult)
+        ts(v("NZ"), v("NN"), 0.0, OP.is_equal)
 
     def slots_a():
         for r in range(16):
             mm(v("pM", 16 * r, 16 * r + 16), srow(r), v("F1", 0, 16))
-        act(v("F0R"), v("pM", 0, 256), scale=32.0)
-        fill(v("J0", 0, 256), 0.0)
-        cp(v("SLW", 0, CAP), v("S512"))
-        tt(v("DZ"), v("NZ"), v("DLP32"), OP.mult)
-        ts(v("PF"), v("F1", 0, 16), 32.0, OP.mult)
-        tt(v("PF"), v("DZ"), v("PF"), OP.add)
+        act(v("F0R"), v("pM", 0, 256))
+        tt(v("DZ"), v("NZ"), v("DLP"), OP.mult)
+        tt(v("PF"), v("DZ"), v("F1", 0, 16), OP.add)
         flip(v("PF"), None, v("JL"))
 
     def slots_b():
@@ -492,28 +494,23 @@ def rank_program(g, core, T, topo):
             expand(64, 96)
             if t == 0:
                 setup_c()
-                numbers(A)
-            widths()
+            widths(t)
             if t:
                 put_course(t - 1)
-            fill(v("ASKW", 0, CAP), 1024.0)
         dist(CUTS, 256, {0: [course], "tail": [setup_d] * (t == 0) + [slots_a]})
 
         def ask():
-            tt(v("XN"), v("P32"), v("NN"), OP.mult)
-            scan(v("SC"), v("XN"), v("ZERO"), OP.add, OP.add)
-            mm(v("pX", 16, 17), v("TRI"), v("SC", 15, 16))
             ts(v("E2"), v("XN"), 0.0, OP.is_equal)
             tt(v("E2"), v("E2"), v("DLP"), OP.mult)
-            tt(v("SX"), v("SC"), v("XN"), OP.subtract)
-            tt(v("SX"), v("SX"), v("E2"), OP.add)
+            tt(v("SX"), v("SC", 0, 16), v("E2"), OP.add)
             flip(v("SX"), v("pX", 16, 17), v("APL"))
             cp(ind(v("ASKW"), v("APL")), v("ZB"))
             send(lender, v("ASKL", CAP * t, CAP * t + CAP), v("ASKW", 0, CAP), "aa%d" % t, "la%d" % t)
             arrives(v("ASKL", CAP * t, CAP * t + CAP), asker, "aa%d" % t)
         choose(256, True, "DC%d" % (t % 2), "LAY", ask)
         cp(ind(v("U", 0, DL), v("LAY")), v("C255"))
-        act(v("TW", A + L, A + 2 * L), ind(v("TW", 0, A + L), v("LAY")))
+        if t < RO - 1:
+            act(v("TW", A + L, A + 2 * L), ind(v("TW", 0, A + L), v("LAY")))
         act(v("NW", A + L, A + 2 * L), ind(v("NW", 0, A + L), v("LAY")))
         z = CAP * t
         hash_a("ASKL", z, CAP)
@@ -531,13 +528,16 @@ def rank_program(g, core, T, topo):
         slots_c()
         ts(v("SLOT"), v("pM", 256, 272), -1.0, OP.add)
         cp(ind(v("U"), v("LEN", 0, 3)), v("C255", 0, 48))
-        fill(v("U", DL, WID), 0.0)
-        act(v("TW", B, B + L), ind(v("TW", A, A + 2 * L), v("SLOT")))
+        if t < RO - 1:
+            act(v("TW", B, B + L), ind(v("TW", A, A + 2 * L), v("SLOT")))
         act(v("NW", B, B + L), ind(v("NW", A, A + 2 * L), v("SLOT")))
-        mm(v("pX", 18, 19), v("ONE"), v("SC", 15, 16))
-        cp(v("PIN"), v("pX", 18, 19))
-        ts(v("PI2"), v("PIN"), 63, OP.bitwise_and)
-        ts(v("THR"), v("PI2"), 16.0, OP.mult, v("TH16"), OP.add)
+        if t < RO - 1:
+            act(v("U", DL, WID), v("KEEP", 0, CAP), scale=0.0)
+            prefill()
+            mm(v("pX", 18, 19), v("ONE"), v("SC", 16, 17))
+            cp(v("PIN"), v("pX", 18, 19))
+            ts(v("PI2"), v("PIN"), 63, OP.bitwise_and)
+            ts(v("THR"), v("PI2"), 32.0, OP.mult, v("TH16"), OP.add)
         r0 = RETN * t
         tt(v("FIX", 0, 3), v("SLS", 15, CAP, 16), v("RETL", r0 + 96, r0 + 99), OP.add)
         if t < RO - 1:
@@ -547,7 +547,6 @@ def rank_program(g, core, T, topo):
     B = S + AREA * (RO % 2)
     cp(ind(v("NW", B, B + AREA), v("FIX", 0, 3)), v("NB", CAP * (RO - 1), CAP * RO))
     numbers(B)
-    cp(v("CI"), v("pM", 272, 288))
     put_course(RO - 1)
     dma("S", T.yu[:, S:S + RO * CAP], v("UB"))
     for s in ("sV", "sA", "sP", "sG"):

from concourse.mybir import AluOpType as OP, ActivationFunctionType as AF

RO, CAP, L, S = 5, 48, 256, 2048
AREA = 560
DL = S + 2 * AREA
WID = DL + CAP
ASKN = 800
RETN = 104

_sb = {
    "U": (WID, "bfloat16"), "TW": (WID, "bfloat16"), "NW": (WID, "bfloat16"), "NH": (S, "bfloat16"),
    "C0L": (16, "int32"), "HWI": (2, "int32"), "KMI": (1, "int32"), "THI": (1, "int32"),
    "PIX": (1, "int32"), "PA_": (1, "int32"), "PG_": (1, "int32"), "COL": (16, "float32"), "SELC": (16, "float32"),
    "GI": (128, "float32"), "YI": (144, "float32"), "AI": (256, "float32"),
    "BO": (128, "bfloat16"), "BOH": (128, "float16"), "IDH": (128, "float16"), "SB": (144, "bfloat16"), "S16": (144, "bfloat16"), "SN": (144, "bfloat16"),
    "S0": (144, "bfloat16"), "S256": (144, "bfloat16"), "SR": (2048, "bfloat16"), "PAM": (128, "bfloat16"), "PBM": (128, "bfloat16"),
    "TRI": (128, "bfloat16"), "SHB": (128, "bfloat16"), "ONE": (128, "bfloat16"), "RST": (256, "float32"), "KEEP": (1024, "bfloat16"), "EA": (336, "float32"),
    "MASK": (256, "bfloat16"), "DLP": (16, "float32"), "DLP32": (16, "float32"), "CL0": (16, "float32"),
    "DC0": (16, "float32"), "DC1": (16, "float32"), "DC2": (16, "float32"), "DD0": (16, "float32"), "DD1": (16, "float32"),
    "DD2": (16, "float32"), "FIXC": (16, "float32"), "FOUR": (16, "float32"),
    "ZERO": (16, "float32"), "CI1": (256, "bfloat16"), "NB": (240, "bfloat16"), "C255": (256, "bfloat16"),
    "S512": (48, "float32"), "E8": (128, "float32"), "THF": (16, "float32"), "TH16": (1, "float32"), "THR": (1, "float32"),
    "WU": (16, "float16"), "WK": (128, "float16"), "WF": (2, "float32"), "WI": (2, "int32"), "KD": (16, "float16"), "KF": (1, "float32"),
    "KI1": (1, "int32"), "KW": (16, "int32"), "KW2": (16, "int32"), "TMPC": (128, "float32"),
    "ZB": (256, "bfloat16"), "UVI": (32, "int32"), "UVM": (32, "int32"), "TT": (16, "int32"), "TSI": (256, "int32"),
    "BO300": (128, "float16"), "TXF": (256, "float16"), "HI": (256, "int32"), "HM": (256, "int32"), "H16": (256, "uint16"),
    "ZS": (1536, "bfloat16"), "ZX": (4096, "bfloat16"), "DF": (4096, "bfloat16"), "KY": (256, "int32"),
    "PQ": (16, "float32"), "XN": (16, "bfloat16"), "SC": (32, "bfloat16"), "SX": (16, "float32"), "E2": (16, "float32"), "PT": (32, "float32"),
    "PU": (32, "float32"), "APL": (16, "uint16"), "ASKW": (ASKN, "bfloat16"), "PIN": (1, "int32"), "PI2": (1, "int32"),
    "MC": (16, "int32"), "P32": (16, "float32"), "NE": (16, "float32"), "CODE": (16, "bfloat16"), "OH": (256, "float16"), "HO": (256, "float16"),
    "HR": (256, "float16"), "M1": (256, "float32"), "LS": (256, "float32"), "EI": (256, "bfloat16"), "EB": (1920, "bfloat16"),
    "EL": (16, "float32"), "HD": (16, "float32"), "HMM": (16, "float32"), "CM": (256, "float32"), "CS": (256, "float32"), "WA": (16, "float32"),
    "WM": (16, "float32"), "LAY": (16, "uint16"), "LEN": (4, "uint16"),
    "CI": (16, "int32"), "CW": (16, "int32"), "CE": (32, "bfloat16"), "CFI": (32, "int32"), "F1": (32, "bfloat16"),
    "NN": (16, "bfloat16"), "NZ": (16, "float32"), "DZ": (16, "float32"), "PF": (16, "float32"), "JL": (16, "uint16"),
    "J0": (ASKN, "bfloat16"), "JM": (256, "bfloat16"), "JF": (256, "bfloat16"), "SLOT": (16, "uint16"),
    "F0R": (256, "float32"), "SLW": (ASKN, "float32"), "SLM": (48, "float32"), "SLS": (48, "float32"), "FIX": (4, "uint16"), "CF": (80, "float32"),
    "ASKL": (RO * CAP, "bfloat16"), "RESP": (RETN, "bfloat16"), "RETL": (RO * RETN, "bfloat16"), "UB": (240, "bfloat16"),
}
_ps = ("pZ", "pUV", "pS", "pD", "pC", "pN", "pX", "pM")
_place = {}
_fill = {}
for _k in _sb:
    if _sb[_k][0] <= 48:
        _d = _sb[_k][1]
        _place[_k] = ("pack_" + _d, _fill.get(_d, 0))
        _fill[_d] = _fill.get(_d, 0) + (_sb[_k][0] + 15) // 16 * 16
SCRATCH = {k: ("sbuf", [128, _sb[k][0]], _sb[k][1]) for k in _sb if k not in _place}
SCRATCH.update({"pack_" + k: ("sbuf", [128, _fill[k]], k) for k in _fill})
SCRATCH.update({k: ("psum", [128, 512], "float32") for k in _ps})
_bytes = {"bfloat16": 2, "float16": 2, "uint16": 2, "float32": 4, "int32": 4}
SEMAPHORES = ["sV", "sA", "sP", "sG"] + ["d%d" % i for i in range(16)] + [a + str(t) for a in ("la", "lr", "aa", "ar") for t in range(RO)]
CUTS = [(0, 64), (64, 96), (96, 160), (160, 208), (208, 240), (240, 256)]


def rank_program(g, core, T, topo):
    rank = T.rank_of(core)
    if rank is None:
        return
    cores = list(T.cores)
    N = len(cores)
    Q = {"V": g.vector, "A": g.scalar, "P": g.tensor, "G": g, "S": g.sync}
    count = {"sV": 0, "sA": 0, "sP": 0, "sG": 0}
    know = {q: {} for q in Q}
    snap = {}
    hist = {}
    ndma = [0]

    def v(b, c0=0, c1=None, st=1, p=128, rows=None):
        p = rows or p
        if b in _place:
            o = _place[b][1]
            return (_place[b][0], o + c0, o + (_sb[b][0] if c1 is None else c1), st, p)
        return (b, c0, (SCRATCH[b][1][1] if c1 is None else c1), st, p)

    def ind(w, o):
        return ("I", w, o)

    def ap(x):
        if x[0] == "I":
            return ap(x[1]).indirect(ap(x[2]))
        b, c0, c1, st, p = x
        t = T[b]
        if isinstance(p, tuple):
            return t[p[0]:p[1]:p[2], c0:c1]
        if st == 1:
            return t[:, c0:c1] if p == 128 else t[0:p, c0:c1]
        return t[:, c0:c1:st] if p == 128 else t[0:p, c0:c1:st]

    def span(x):
        n = _bytes[SCRATCH[x[0]][2]]
        return x[0], x[1] * n // 16, (x[2] * n + 15) // 16

    def learn(q, sem, val):
        k = know[q]
        if k.get(sem, 0) >= val:
            return
        k[sem] = val
        for s2, v2 in snap.get((sem, val), {}).items():
            if k.get(s2, 0) < v2:
                k[s2] = v2

    def need(q, rd, wr):
        deps = {}
        for x, w in [(x, False) for x in rd] + [(x, True) for x in wr]:
            b, lo, hi = span(x)
            ps = SCRATCH[b][0] == "psum"
            keep = []
            for e in hist.get(b, []):
                elo, ehi, ew, eq, es, ev = e
                hit = (ps and eq != q) or (not ps and elo < hi and lo < ehi)
                if hit and (w or ew or ps):
                    if deps.get(es, 0) < ev:
                        deps[es] = ev
                    if ps or (w and lo <= elo and ehi <= hi):
                        continue
                keep.append(e)
            hist[b] = keep
        for s in sorted(deps):
            if know[q].get(s, 0) < deps[s]:
                Q[q].wait_ge(T.sem[s], deps[s])
                learn(q, s, deps[s])

    def note(q, rd, wr, sem, val):
        snap[(sem, val)] = dict(know[q])
        for x, w in [(x, False) for x in rd] + [(x, True) for x in wr]:
            b, lo, hi = span(x)
            h = hist.setdefault(b, [])
            h[:] = [e for e in h if not (e[0] == lo and e[1] == hi and e[2] == w and e[3] == q and e[4] == sem)]
            h.append((lo, hi, w, q, sem, val))

    def a_(x):
        return ap(x) if isinstance(x, tuple) else x

    def run(q, out, ins, f):
        rd, wr = [], []
        for x in ins:
            if isinstance(x, tuple):
                rd += [x[1], x[2]] if x[0] == "I" else [x]
        if out[0] == "I":
            wr.append(out[1])
            rd.append(out[2])
        else:
            wr.append(out)
        need(q, rd, wr)
        s = "s" + q
        count[s] += 1
        f().then_inc(T.sem[s], 1)
        note(q, rd, wr, s, count[s])

    def cp(out, in_):
        run("V", out, [in_], lambda: g.vector.tensor_copy(out=ap(out), in_=ap(in_)))

    def tt(out, a, b, op):
        run("V", out, [a, b], lambda: g.vector.tensor_tensor(out=ap(out), in0=ap(a), in1=ap(b), op=op))

    def ts(out, a, s1, op0, s2=None, op1=None):
        if op1 is None:
            run("V", out, [a, s1], lambda: g.vector.tensor_scalar(out=ap(out), in0=ap(a), scalar1=a_(s1), scalar2=None, op0=op0))
        else:
            run("V", out, [a, s1, s2], lambda: g.vector.tensor_scalar(out=ap(out), in0=ap(a), scalar1=a_(s1), scalar2=a_(s2), op0=op0, op1=op1))

    def scan(out, d0, d1, op0, op1):
        run("V", out, [d0, d1], lambda: g.vector.tensor_tensor_scan(out=ap(out), data0=ap(d0), data1=ap(d1), initial=0.0, op0=op0, op1=op1))

    def fill(out, c):
        run("V", out, [], lambda: g.vector.memset(ap(out), c))

    def act(out, in_, func=AF.Copy, scale=1.0, bias=0.0):
        run("A", out, [in_, scale, bias], lambda: g.scalar.activation(out=ap(out), in_=ap(in_), func=func, bias=a_(bias), scale=a_(scale)))

    def mm(out, lhsT, rhs, start=True, stop=True):
        run("P", out, [lhsT, rhs], lambda: g.tensor.matmul(ap(out), ap(lhsT), ap(rhs), start=start, stop=stop))

    def iota(out, pat, base=0, cm=0):
        if SCRATCH[out[0]][2] != "int32":
            run("G", out, [], lambda: g.iota(ap(out), pat, base, cm, allow_small_or_imprecise_dtypes=True))
        else:
            run("G", out, [], lambda: g.iota(ap(out), pat, base, cm))

    def dma(q, out, in_):
        rd = [in_] if isinstance(in_, tuple) else []
        wr = [out] if isinstance(out, tuple) else []
        need(q, rd, wr)
        s = "d%d" % ndma[0]
        ndma[0] += 1
        Q[q].dma_start(out=a_(out), in_=a_(in_)).then_inc(T.sem[s], 16)
        snap[(s, 16)] = dict(know[q])
        for x, w in [(x, False) for x in rd] + [(x, True) for x in wr]:
            b, lo, hi = span(x)
            hist.setdefault(b, []).append((lo, hi, w, "dma", s, 16))

    def engs(src, dst):
        return topo.engines(src, dst)[:8]

    def send(dst, out, in_, rsem, lsem):
        need("G", [in_], [])
        mask = 0
        for e in engs(core, dst):
            mask |= 1 << e
        rid, pid = topo.addr(dst, core)
        g.remote_dma(ap(out), ap(in_), T.sem[rsem], T.sem[lsem], pid, rid, mask)
        b, lo, hi = span(in_)
        hist.setdefault(b, []).append((lo, hi, False, "rdma", lsem, len(engs(core, dst))))
        snap[(lsem, len(engs(core, dst)))] = dict(know["G"])

    def arrives(x, src, rsem):
        b, lo, hi = span(x)
        hist.setdefault(b, []).append((lo, hi, True, "rdma", rsem, len(engs(src, core))))

    dma("S", v("C0L"), T.c0[:])
    dma("S", v("TW", 0, S), T.tp[:])
    dma("A", v("HWI"), T.hw[:])
    dma("A", v("KMI"), T.km[:])
    dma("A", v("THI", p=8), T.th[:])
    dma("A", v("U", 0, S), T.us[:])
    iota(v("PIX"), [[0, 1]], 0, 1)
    iota(v("GI"), [[1, 8], [0, 16]])
    iota(v("AI"), [[0, 16], [1, 16]])
    iota(v("YI"), [[1, 144]])
    iota(v("CL0"), [[16, 16]])
    iota(v("NW", 0, S), [[0, 128], [1, 16]])
    iota(v("NH"), [[1, 128], [0, 16]])
    dma("S", v("NW", 0, S, rows=(0, 128, 16)), v("NH", 0, S, rows=(0, 8, 1)))
    iota(v("CI1"), [[1, 256]], 1)
    iota(v("S512"), [[1, 48]], 256)
    iota(v("NB"), [[0, 15], [1, 16]])
    iota(v("NH", 0, 240), [[1, 15], [0, 16]], 128)
    dma("S", v("NB", rows=(0, 128, 16)), v("NH", 0, 240, rows=(0, 8, 1)))
    PIX, PA, PG = v("PIX"), v("PA_"), v("PG_")

    def col(i):
        return v("COL", i, i + 1)
    ts(PA, PIX, 15, OP.bitwise_and)
    ts(PG, PIX, 4, OP.arith_shift_right)
    cp(col(0), PA)
    cp(col(1), PG)
    cp(col(3), PIX)
    GI, YI = v("GI"), v("YI", 0, 128)
    ts(v("BO"), GI, col(1), OP.is_equal)
    ts(v("SELC"), v("AI", 0, 16), col(0), OP.is_equal)
    for j in range(4):
        act(v("KEEP", 256 * j, 256 * j + 256), v("AI"), AF.Sign)
    act(v("ZS", 0, 1024), v("KEEP"), scale=0.0)
    act(v("ZS", 1024, 1536), v("KEEP", 0, 512), scale=0.0)
    ts(PA, PIX, 4, OP.arith_shift_right)
    ts(PG, PA, 1, OP.bitwise_and)
    cp(col(6), PG)
    ts(col(5), col(6), -1.0, OP.mult, 1.0, OP.add)
    cp(v("BOH"), v("BO"))
    ts(col(7), col(0), 8.0, OP.is_ge)
    ts(col(8), col(7), -1.0, OP.mult, 1.0, OP.add)
    ts(col(9), col(3), -8.0, OP.add)
    ts(col(10), col(3), 8.0, OP.add)
    act(v("RST"), v("KEEP", 0, 256), scale=-1048578.0, bias=1048576.0)
    ts(col(2), col(1), 16.0, OP.mult, 15.0, OP.add)
    ts(v("SB"), v("YI"), col(2), OP.is_equal)
    ts(col(11), col(0), 0.0, OP.is_equal)
    ts(col(12), col(0), 1.0, OP.is_equal)
    ts(col(13), col(11), 16.0, OP.mult)
    tt(col(13), col(13), col(12), OP.add)
    act(v("S16"), v("SB"), scale=32.0)
    act(v("SN"), v("SB"), scale=col(13))
    act(v("S0"), v("SB"), scale=col(11))
    act(v("S256"), v("S0"), scale=256.0)
    for r in range(16):
        act(v("SR", 128 * r, 128 * r + 128), v("BO"), scale=v("SELC", r, r + 1))
    cp(v("SX"), v("C0L"))

    def flip(src, off, lst):
        for h in (0, 1):
            if off is None:
                ts(v("PT", 16 * h, 16 * h + 16), src, col(5 + h), OP.mult)
            else:
                ts(v("PT", 16 * h, 16 * h + 16), src, off, OP.add, col(5 + h), OP.mult)
        run("V", v("PU"), [v("PT")], lambda: g.vector.transpose(out=ap(v("PU")), in_=ap(v("PT"))))
        tt(lst, v("PU", 0, 16), v("PU", 16, 32), OP.add)
    flip(v("SX"), None, v("JL"))
    ts(v("PAM"), YI, col(9), OP.is_equal, col(7), OP.mult)
    ts(v("PBM"), YI, col(10), OP.is_equal, col(8), OP.mult)
    ts(v("WI"), v("HWI"), 2047, OP.bitwise_and)
    cp(v("WF"), v("WI"))
    for i in (0, 1):
        ts(v("WU", 8 * i, 8 * i + 8), v("GI", 0, 128, 16), col(1), OP.is_equal, v("WF", i, i + 1), OP.mult)
    ts(v("KI1"), v("KMI"), 2047, OP.bitwise_and)
    cp(v("KF"), v("KI1"))
    ts(v("KD"), v("AI", 0, 16), col(0), OP.is_equal, v("KF"), OP.mult)
    mm(v("pX", 0, 16), v("BOH"), v("KD"))
    ts(v("KW"), v("pX", 0, 16), v("WF", 0, 1), OP.mult)
    ts(v("KW2"), v("KW"), 2047, OP.bitwise_and)
    for j in range(8):
        tt(v("WK", 16 * j, 16 * j + 16), v("KW2"), v("BO", 16 * j, 16 * j + 16), OP.mult)
    ts(v("IDH"), YI, col(3), OP.is_equal)
    ts(v("TSI"), v("AI"), 0.0, OP.mult)
    A0 = S
    cp(v("TW", A0, A0 + L), ind(v("TW", 0, S), v("JL")))

    def sel(b, r):
        return v(b, 15 - r, 143 - r)

    def srow(r):
        return v("SR", 128 * r, 128 * r + 128)

    def setup_b():
        act(v("NW", A0, A0 + L), ind(v("NW", 0, S), v("JL")))
        act(v("NW", A0 + L, WID), v("KEEP", 0, WID - A0 - L), scale=0.0)
        act(v("TW", A0 + L, WID), v("KEEP", 0, WID - A0 - L), scale=0.0)
        prefill()
        fill(v("U", S, WID), 0.0)

    def prefill():
        act(v("ASKW", 0, CAP), v("KEEP", 0, CAP), scale=0.0, bias=1024.0)
        act(v("SLW", 0, CAP), v("S512"))
        act(v("J0", 0, 256), v("KEEP", 0, 256), scale=0.0)

    def setup_c():
        cp(v("THF", 0, 1, p=8), v("THI", p=8))
        ts(v("E8", p=8), v("GI", p=8), v("COL", 3, 4, p=8), OP.is_equal)
        mm(v("pX", 16, 17), v("E8", p=8), v("THF", 0, 1, p=8))
        ts(v("TH16"), v("pX", 16, 17), 32.0, OP.mult, -30.0, OP.add)
        cp(v("THR"), v("TH16"))
        ts(v("TMPC"), v("AI", 0, 128), col(0), OP.is_gt)
        tt(v("TRI"), v("TMPC"), v("BO"), OP.mult)
        ts(col(14), col(0), 16.0, OP.mult)
        ts(v("DLP"), v("AI", 0, 16), col(14), OP.add, 272.0, OP.add)
        ts(v("FOUR"), v("DLP"), 272.0 + 254.0, OP.is_equal, 1600.0, OP.mult)
        ts(v("FOUR"), v("FOUR"), 4.0, OP.add)
        fill(v("ZERO"), 0.0)
        fill(v("CE", 0, 1), 0.0)
        fill(v("SC", 0, 1), 0.0)

    def setup_d():
        ts(v("MASK"), v("AI"), col(0), OP.is_equal)
        ts(PA, PIX, 1, OP.add)
        ts(PG, PA, 15, OP.bitwise_and)
        ts(col(4), PG, 2.0, OP.mult)
        ts(v("BO300"), v("BO"), 300.0, OP.mult)
        ts(v("DC0"), v("CL0"), col(0), OP.add, float(S), OP.add)
        ts(v("DC1"), v("DC0"), float(AREA), OP.add)
        ts(v("DC2"), v("DC0"), float(DL - S), OP.add)
        for i in "012":
            ts(v("DD" + i), v("DC" + i), 1.0, OP.add)
        fill(v("C255"), 255.0)
        fill(v("ONE"), 1.0)
        fill(v("RESP"), 0.0)

    def hash_a(z, zc, n):
        m = min(n, 128)
        nb = (n + 127) // 128
        for b in range(nb):
            for i in (0, 1):
                mm(v("pUV", 16 * i + 8 * b, 16 * i + 8 * b + 8, p=m), v(z, zc + 128 * b, zc + 128 * b + m), v("WU", 8 * i, 8 * i + 8))
        mm(v("pS", 0, n), v("WK"), v(z, zc, zc + n), True, False)
        cp(v("UVI", p=m), v("pUV", 0, 32, p=m))
        ts(v("UVM", p=m), v("UVI", p=m), 2047, OP.bitwise_and)
        tt(v("TT", p=m), v("UVM", 0, 16, p=m), v("UVM", 16, 32, p=m), OP.mult)
        k = 8 * nb
        ts(v("TSI", 0, 16 * k, 16, p=m), v("TT", 0, k, p=m), 5, OP.arith_shift_right, 2047, OP.bitwise_and)
        scan(v("TXF", 0, 16 * k, p=m), v("KEEP", 0, 16 * k, p=m), v("TSI", 0, 16 * k, p=m), OP.mult, OP.add)
        for b in range(nb):
            mm(v("pS", 128 * b, 128 * b + m), v("TXF", 128 * b, 128 * b + 128, p=m), v("IDH", 0, m, p=m), False, b == nb - 1)

    def hash_b(n):
        cp(v("HI", 0, n), v("pS", 0, n))
        ts(v("HM", 0, n), v("HI", 0, n), 2047, OP.bitwise_and)
        cp(v("H16", 0, n), v("HM", 0, n))

    def expand(k0, k1):
        scan(v("ZX", 16 * k0, 16 * k1), v("KEEP", 0, 16 * (k1 - k0)), v("ZS", 16 * k0, 16 * k1), OP.mult, OP.add)

    def dist(cuts, n, hooks):
        for i, (k0, k1) in enumerate(cuts):
            x = v("DF", 16 * k0, 16 * k1)
            tt(x, ind(v("U", 0, S), v("H16", k0, k1)), v("ZX", 16 * k0, 16 * k1), OP.subtract)
            act(x, x, AF.Abs)
            for h in hooks.get(i, ()):
                h()
            for r in range(k0 // 16, k1 // 16):
                mm(v("pD", 0, 256), sel("S16", r), v("DF", 256 * r, 256 * r + 256), r == 0, r == n // 16 - 1)
        for h in hooks.get("tail", ()):
            h()
        scan(v("KY"), v("RST"), v("pD", 0, 256), OP.add, OP.min)

    KEY = v("KY", 15, 256, 16)

    def choose(n, own, dc, lst, hook):
        k = n // 16
        ts(v("PQ"), KEY, v("THR"), OP.is_ge)
        if own:
            tt(v("XN"), v("PQ"), v("NN"), OP.mult)
            scan(v("SC", 1, 17), v("XN"), v("ZERO"), OP.add, OP.add)
            mm(v("pX", 16, 17), v("TRI"), v("SC", 16, 17))
        ts(v("MC"), KEY, 30, OP.bitwise_and)
        if own:
            tt(v("NE"), v("PQ"), v("NZ"), OP.max)
        tt(v("CODE"), v("NE") if own else v("PQ"), v("MC"), OP.add)
        for r in range(k):
            mm(v("pC", 16 * r, 16 * r + 16), srow(r), v("CODE"))
        hook()
        ts(v("OH", 0, n), v("pC", 0, n), col(4), OP.is_equal)
        tt(v("HO", 0, n), v("OH", 0, n), v("HM", 0, n), OP.mult)
        h1 = v("pC", 256, 256 + n)
        mm(h1, v("BOH"), v("OH", 0, n), True, False)
        mm(h1, v("BOH"), v("HO", 0, n), False, True)
        mm(v("pN", 0, n), v("BO300"), v("OH", 0, n), True, False)
        tt(v("M1", 0, n), h1, v("MASK", 0, n), OP.mult)
        cp(v("HR", 0, n), h1)
        scan(v("LS", 0, n), v("KEEP", 0, n), v("M1", 0, n), OP.mult, OP.add)
        tt(v("EI", 0, n), h1, v("LS", 0, n), OP.is_equal)
        mm(v("pN", 0, n), v("BO"), v("EI", 0, n), False, False)
        kv = 11 if own else k - 1
        o = [0]
        for c in range(k - 1):
            o.append(o[c] + n - 16 * (c + 1))
        for c in range(kv, k - 1):
            act(v("EA", o[c] - o[kv], o[c + 1] - o[kv]), v("pC", 256 + 16 * (c + 1), 256 + n), AF.Abs, -1.0, v("LS", 16 * c + 15, 16 * c + 16))
        if kv < k - 1:
            act(v("EB", o[kv], o[k - 1]), v("EA", 0, o[k - 1] - o[kv]), AF.Relu, -1.0, 1.0)
        for c in range(k - 1):
            if c < kv:
                ts(v("EB", o[c], o[c + 1]), v("HR", 16 * (c + 1), n), v("LS", 16 * c + 15, 16 * c + 16), OP.is_equal)
            mm(v("pN", 16 * (c + 1), n), v("BO"), v("EB", o[c], o[c + 1]), False, c == k - 2)
        HL = v("LS", 15, n, 16)
        tt(v("HD", 0, k), HL, v("DD" + dc[2], 0, k), OP.subtract)
        tt(v("CM", 0, n), v("pN", 0, n), v("MASK", 0, n), OP.mult)
        scan(v("CS", 0, n), v("KEEP", 0, n), v("CM", 0, n), OP.mult, OP.add)
        ts(v("WA", 0, k), v("CS", 15, n, 16), 301.0, OP.is_equal)
        tt(v("WM", 0, k), v("WA", 0, k), v("HD", 0, k), OP.mult)
        tt(v(lst, 0, k), v("WM", 0, k), v(dc, 0, k), OP.add)

    def numbers(A):
        for r in range(16):
            mm(v("pM", 272, 288), sel("SN", r), v("NW", A + 16 * r, A + 16 * r + 16), r == 0, r == 15)

    def put_course(t):
        act(v("CF", 16 * t, 16 * t + 16), v("pM", 272, 288))
        dma("S", T.yc[:, 256 * t:256 * t + 256], v("CF", 16 * t, 16 * t + 16))

    def widths(t):
        if t:
            cp(v("CI"), v("pM", 272, 288))
        ts(v("CW"), v("CI") if t else v("C0L"), 3, OP.bitwise_and)
        scan(v("CE", 1, 17), v("CW"), v("FOUR"), OP.add, OP.add)
        mm(v("pX", 16, 17), v("TRI"), v("CE", 16, 17))
        ts(v("CFI", 0, 17), v("CE", 0, 17), v("pX", 16, 17), OP.add, 0.2, OP.mult)
        ts(v("F1", 0, 17), v("CFI", 0, 17), 256.0, OP.min)
        tt(v("NN"), v("F1", 1, 17), v("F1", 0, 16), OP.subtract)
        ts(v("NZ"), v("NN"), 0.0, OP.is_equal)

    def slots_a():
        for r in range(16):
            mm(v("pM", 16 * r, 16 * r + 16), srow(r), v("F1", 0, 16))
        act(v("F0R"), v("pM", 0, 256))
        tt(v("DZ"), v("NZ"), v("DLP"), OP.mult)
        tt(v("PF"), v("DZ"), v("F1", 0, 16), OP.add)
        flip(v("PF"), None, v("JL"))

    def slots_b():
        cp(ind(v("J0"), v("JL")), v("CI1"))
        scan(v("JM"), v("J0", 0, 256), v("J0", 0, 256), OP.max, OP.max)
        act(v("JF"), v("J0", 0, 256), AF.Sign)

    def slots_m():
        for b, x in (("S0", "JM"), ("S256", "JF")):
            for p in range(16):
                mm(v("pM", 256, 272), sel(b, p), v(x, p, 256, 16), b == "S0" and p == 0, b == "S256" and p == 15)

    def slots_c():
        cp(ind(v("SLW"), v("APL")), v("F0R"))
        tt(v("SLM"), v("SLW", 0, CAP), v("MASK", 0, CAP), OP.mult)
        scan(v("SLS"), v("KEEP", 0, CAP), v("SLM"), OP.mult, OP.add)

    for t in range(RO):
        A = S + AREA * (t % 2)
        B = S + AREA * (1 - t % 2)
        lender = cores[(rank + 1 + t % (N - 1)) % N]
        asker = cores[(rank - 1 - t % (N - 1)) % N]
        mm(v("pZ", 0, 256), v("PAM"), v("TW", A, A + L), True, False)
        mm(v("pZ", 0, 255), v("PBM"), v("TW", A + 1, A + L), False, True)
        cp(v("ZB"), v("pZ", 0, 256))
        for m in range(16):
            act(v("ZX", 1536 + m, 4096, 16), v("ZB", 96, 256))
        cp(v("ZS", 0, 1536, 16), v("ZB", 0, 96))
        hash_a("ZB", 0, 256)
        if t == 0:
            setup_b()
        else:
            cp(ind(v("NW", A, A + AREA), v("FIX", 0, 3)), v("NB", CAP * (t - 1), CAP * t))
            numbers(A)
        expand(0, 64)
        hash_b(256)

        def course():
            expand(64, 96)
            if t == 0:
                setup_c()
            widths(t)
            if t:
                put_course(t - 1)
        dist(CUTS, 256, {0: [course], "tail": [setup_d] * (t == 0) + [slots_a]})

        def ask():
            ts(v("E2"), v("XN"), 0.0, OP.is_equal)
            tt(v("E2"), v("E2"), v("DLP"), OP.mult)
            tt(v("SX"), v("SC", 0, 16), v("E2"), OP.add)
            flip(v("SX"), v("pX", 16, 17), v("APL"))
            cp(ind(v("ASKW"), v("APL")), v("ZB"))
            send(lender, v("ASKL", CAP * t, CAP * t + CAP), v("ASKW", 0, CAP), "aa%d" % t, "la%d" % t)
            arrives(v("ASKL", CAP * t, CAP * t + CAP), asker, "aa%d" % t)
        choose(256, True, "DC%d" % (t % 2), "LAY", ask)
        cp(ind(v("U", 0, DL), v("LAY")), v("C255"))
        if t < RO - 1:
            act(v("TW", A + L, A + 2 * L), ind(v("TW", 0, A + L), v("LAY")))
        act(v("NW", A + L, A + 2 * L), ind(v("NW", 0, A + L), v("LAY")))
        z = CAP * t
        hash_a("ASKL", z, CAP)
        cp(v("ZS", 0, 16 * CAP, 16), v("ASKL", z, z + CAP))
        expand(0, CAP)
        hash_b(CAP)
        dist([(0, 32), (32, 48)], CAP, {"tail": [slots_b]})
        choose(CAP, False, "DC2", "LEN", lambda: None)
        slots_m()
        act(v("RESP", 48, 96), ind(v("TW"), v("LEN", 0, 3)))
        cp(v("RESP", 0, 48), ind(v("U"), v("LEN", 0, 3)))
        ts(v("RESP", 96, 99), v("LEN", 0, 3), float(DL), OP.is_ge, 256.0, OP.mult)
        send(asker, v("RETL", RETN * t, RETN * t + RETN), v("RESP"), "ar%d" % t, "lr%d" % t)
        arrives(v("RETL", RETN * t, RETN * t + RETN), lender, "ar%d" % t)
        slots_c()
        ts(v("SLOT"), v("pM", 256, 272), -1.0, OP.add)
        cp(ind(v("U"), v("LEN", 0, 3)), v("C255", 0, 48))
        if t < RO - 1:
            act(v("TW", B, B + L), ind(v("TW", A, A + 2 * L), v("SLOT")))
        act(v("NW", B, B + L), ind(v("NW", A, A + 2 * L), v("SLOT")))
        if t < RO - 1:
            act(v("U", DL, WID), v("KEEP", 0, CAP), scale=0.0)
            prefill()
            mm(v("pX", 18, 19), v("ONE"), v("SC", 16, 17))
            cp(v("PIN"), v("pX", 18, 19))
            ts(v("PI2"), v("PIN"), 63, OP.bitwise_and)
            ts(v("THR"), v("PI2"), 32.0, OP.mult, v("TH16"), OP.add)
        r0 = RETN * t
        tt(v("FIX", 0, 3), v("SLS", 15, CAP, 16), v("RETL", r0 + 96, r0 + 99), OP.add)
        if t < RO - 1:
            cp(ind(v("TW", B, B + AREA), v("FIX", 0, 3)), v("RETL", r0 + 48, r0 + 96))
        act(v("UB", CAP * t, CAP * t + CAP), v("RETL", r0, r0 + 48))
    dma("S", T.yu[:, 0:S], v("U", 0, S))
    B = S + AREA * (RO % 2)
    cp(ind(v("NW", B, B + AREA), v("FIX", 0, 3)), v("NB", CAP * (RO - 1), CAP * RO))
    numbers(B)
    put_course(RO - 1)
    dma("S", T.yu[:, S:S + RO * CAP], v("UB"))
    for s in ("sV", "sA", "sP", "sG"):
        g.wait_ge(T.sem[s], count[s])
    for i in range(ndma[0]):
        g.sync.wait_ge(T.sem["d%d" % i], 16)
    for t in range(RO):
        lender = cores[(rank + 1 + t % (N - 1)) % N]
        asker = cores[(rank - 1 - t % (N - 1)) % N]
        for s, n in (("la", len(engs(core, lender))), ("lr", len(engs(core, asker))), ("aa", len(engs(asker, core))), ("ar", len(engs(lender, core)))):
            g.wait_ge(T.sem[s + str(t)], n)
